import numpy as np
import ml_dtypes


def mxq(x, axis, fmt="e4m3"):
    dtype, down = {"e4m3": (ml_dtypes.float8_e4m3fn, 7), "e5m2": (ml_dtypes.float8_e5m2, 14)}[fmt]
    v = np.moveaxis(np.asarray(x, np.float32).astype(ml_dtypes.bfloat16).astype(np.float64), axis, -1)
    blocks = v.reshape(v.shape[:-1] + (-1, 32))
    amax = np.abs(blocks).max(-1, keepdims=True)
    byte = np.maximum(np.where(amax > 0, np.frexp(amax)[1] - 1 + 127, 0) - down, 1)
    scale = np.exp2(byte - 127.0)
    codes = (blocks / scale).astype(np.float32).astype(dtype).astype(np.float64)
    return np.moveaxis((codes * scale).reshape(v.shape), -1, axis)


WIDE = False


def mx_kscale(k):
    if not WIDE:
        return np.ones(k)
    levels = np.array([10, -10, 5, -5, 0])
    if k % 512:
        return np.exp2(np.random.permutation(np.resize(levels, k // 32))).repeat(32)
    a = np.empty((k // 512, 16))
    for p in range(k // 512):
        a[p, :8] = np.random.permutation(np.resize(levels, 8))
        for g in range(8):
            far = levels[np.abs(levels - a[p, g]) >= 10]
            a[p, g + 8] = far[np.random.randint(len(far))]
    return np.exp2(a.ravel()).repeat(32)


BF16 = ml_dtypes.bfloat16


def bf(x):
    return np.asarray(x, np.float32).astype(BF16)


def f64(x):
    return np.asarray(x).astype(np.float64)


B, S, Q, C, P = 512, 1024, 2048, 512, 1024


def sigmoid(z):
    return 0.5 * (1.0 + np.tanh(0.5 * z))


def setup_inputs():
    s, r, t = mx_kscale(S), mx_kscale(C), mx_kscale(P)
    return {"sens": bf(np.random.standard_normal((B, S)) * s),
            "w_val": bf(np.random.standard_normal((S, P)) / np.sqrt(S) / s[:, None] * t),
            "c_val": bf(0.3 * np.random.standard_normal(P) * t),
            "w_gate": bf(np.random.standard_normal((S, P)) / np.sqrt(S) / s[:, None]),
            "c_gate": bf(0.5 * np.random.standard_normal(P)),
            "feat": bf(np.random.standard_normal((Q, C)) * r),
            "w_trunk": bf(np.random.standard_normal((C, P)) / np.sqrt(C) / r[:, None]),
            "c_trunk": bf(0.3 * np.random.standard_normal(P)),
            "slope": bf(1.0 + 0.1 * np.random.standard_normal(P)),
            "amp": bf((1.0 + 0.1 * np.random.standard_normal(P)) / t),
            "dist": bf(np.random.uniform(0.3, 1.5, Q)),
            "lift": bf(0.3 * np.random.standard_normal(Q))}


def reference(sens, w_val, c_val, w_gate, c_gate, feat, w_trunk, c_trunk, slope, amp, dist, lift):
    xq = mxq(f64(sens), 1, "e4m3")
    val = (xq @ mxq(f64(w_val), 0, "e4m3")) + f64(c_val)
    gate = sigmoid((xq @ mxq(f64(w_gate), 0, "e4m3")) + f64(c_gate))
    beta = val * gate
    z = (mxq(f64(feat), 1, "e4m3") @ mxq(f64(w_trunk), 0, "e4m3")) + f64(c_trunk)
    tau = f64(amp) * np.tanh(f64(slope) * z)
    field = mxq(beta, 1, "e4m3") @ mxq(tau, 1, "e4m3").T
    return f64(lift) + f64(dist) * field / np.sqrt(P)

@@ -1,0 +1,414 @@
+from contextlib import ExitStack
+
+import concourse.mybir as mybir
+from concourse.masks import make_identity
+
+B, S, Q, C, P = 512, 1024, 2048, 512, 1024
+FLOPS = 2 * (2 * B * S * P + Q * C * P + B * P * Q)
+
+F32 = mybir.dt.float32
+BF16 = mybir.dt.bfloat16
+U32 = mybir.dt.uint32
+U8 = mybir.dt.uint8
+FP8X4 = mybir.dt.float8_e4m3fn_x4
+ACT = mybir.ActivationFunctionType
+ALU = mybir.AluOpType
+
+NP = 128
+KP = 512
+W = 512
+
+
+def tile_gated_deeponet_meet_f5_kernel(
+    tc, sens, w_val, c_val, w_gate, c_gate, feat, w_trunk, c_trunk, slope, amp, dist, lift, out
+):
+    nc = tc.nc
+    sync, scalar, vector, gpsimd, tensor = nc.sync, nc.scalar, nc.vector, nc.gpsimd, nc.tensor
+    with ExitStack() as ctx:
+        keep = ctx.enter_context(tc.tile_pool(name="keep", bufs=1))
+        work = ctx.enter_context(tc.tile_pool(name="work", bufs=1))
+        psum = ctx.enter_context(tc.psum_pool(name="psum", bufs=8))
+        ctx.enter_context(tc.manual_schedule())
+
+        weights = {"t": w_trunk, "v": w_val, "g": w_gate}
+        raw, grouped, codes, scales = {}, {}, {}, {}
+        act32, bank, turned = {}, {}, {}
+
+        ident32 = keep.tile([NP, NP], F32, name="ident32")
+        ident16 = keep.tile([NP, NP], BF16, name="ident16")
+        mode_rows = keep.tile([NP, KP], BF16, name="mode_rows")
+        mode_rows_t = keep.tile([NP, KP], BF16, name="mode_rows_t")
+        query_rows = keep.tile([NP, NP], BF16, name="query_rows")
+        mode_vec = keep.tile([NP, 16, 4], F32, name="mode_vec")
+        tanh_bias = keep.tile([NP, 2, 4], F32, name="tanh_bias")
+        query_vec = keep.tile([NP, 32], F32, name="query_vec")
+        dist_scaled = keep.tile([NP, 16], F32, name="dist_scaled")
+        warm = keep.tile([NP, 8], F32, name="warm")
+        warm_out = keep.tile([NP, 8], F32, name="warm_out")
+        C_TRUNK, SLOPE, AMP, C_VAL, C_GATE = 0, 2, 4, 6, 8
+
+        def new_bank(dtype=F32):
+            return psum.tile([NP, W if dtype == F32 else 2 * W], dtype, name="bank", tag="bank")
+
+        def new_grouped(key):
+            grouped[key] = work.tile([NP, 4 * W], BF16, name="grouped", tag="grouped", bufs=6, align_bytes=64)
+            return grouped[key]
+
+        def new_act32(key):
+            act32[key] = work.tile([NP, 4, W], F32, name="act32", tag="act32", bufs=8)
+            return act32[key]
+
+        def load_weight(eng, w, s, g):
+            raw[w, s, g] = work.tile([NP, 4, W], BF16, name="raw", tag="raw", bufs=9)
+            src = weights[w][KP * s : KP * (s + 1), W * g : W * (g + 1)]
+            eng.dma_start(out=raw[w, s, g][:], in_=src.rearrange("(p j) c -> p j c", j=4))
+
+        def load_feat(eng, c):
+            raw["f", c] = work.tile([NP, 2, 2 * KP], BF16, name="raw", tag="raw", bufs=9)
+            src = feat[W * c : W * (c + 1), :]
+            eng.dma_start(out=raw["f", c][:], in_=src.rearrange("(h p n) k -> p h (n k)", h=2, n=2))
+
+        def load_sens(eng, h):
+            raw["s", h] = work.tile([NP, 2, S], BF16, name="raw", tag="raw", bufs=9)
+            src = sens[256 * h : 256 * (h + 1), :]
+            eng.dma_start(out=raw["s", h][:], in_=src.rearrange("(n p) k -> p n k", p=NP))
+
+        def clear(eng, which):
+            eng.memset({"mode": mode_rows_t, "query": query_rows, "warm": warm}[which][:], 0.0)
+
+        def load_mode_rows(eng, row):
+            vec = {C_TRUNK: c_trunk, SLOPE: slope, AMP: amp, C_VAL: c_val, C_GATE: c_gate}[row]
+            eng.dma_start(out=mode_rows[row : row + 2, :], in_=vec.rearrange("(g k) -> g k", g=2))
+
+        def load_query_rows(eng, row):
+            vec = {0: dist, 16: lift}[row]
+            eng.dma_start(out=query_rows[row : row + 16, :], in_=vec.rearrange("(n p) -> n p", p=NP))
+
+        def warm_up(eng):
+            eng.activation(out=warm_out[:], in_=warm[:], func=ACT.Sigmoid)
+
+        def identity32(eng):
+            make_identity(nc, ident32[:])
+
+        def identity16(eng):
+            make_identity(nc, ident16[:])
+
+        def copy_on(eng, dst, src):
+            if eng is scalar:
+                eng.copy(out=dst, in_=src)
+            else:
+                eng.tensor_copy(out=dst, in_=src)
+
+        def order_mode_rows(eng):
+            dst = mode_rows_t[0:10, :].rearrange("r (t a i) -> r t a i", t=4, i=4)
+            copy_on(eng, dst, mode_rows[0:10, :].rearrange("r (a t i) -> r t a i", t=4, i=4))
+
+        def turn_mode_rows(eng):
+            bank["mode"] = new_bank(BF16)
+            for t in range(4):
+                cols = slice(NP * t, NP * (t + 1))
+                eng.transpose(bank["mode"][:, cols], mode_rows_t[:, cols], ident16[:])
+
+        def gather_mode(eng):
+            copy_on(eng, mode_vec[:], bank["mode"][:, 0:W].rearrange("p (t r) -> p r t", t=4)[:, 0:16, :])
+
+        def make_tanh_bias(eng):
+            eng.tensor_tensor(
+                out=tanh_bias[:], in0=mode_vec[:, SLOPE : SLOPE + 2, :], in1=mode_vec[:, C_TRUNK : C_TRUNK + 2, :], op=ALU.mult
+            )
+
+        def turn_query_rows(eng):
+            bank["query"] = new_bank(BF16)
+            eng.transpose(bank["query"][:, 0:NP], query_rows[:], ident16[:])
+
+        def gather_query(eng):
+            eng.activation(out=dist_scaled[:], in_=bank["query"][:, 0:16], func=ACT.Copy, scale=1.0 / 32.0)
+            eng.copy(out=query_vec[:, 16:32], in_=bank["query"][:, 16:32])
+
+        def interleave(eng, w, s, g, t0, t1):
+            if (w, s, g) not in grouped:
+                new_grouped((w, s, g))
+            dst = grouped[w, s, g][:].rearrange("p (t a i j) -> p t a j i", t=4, i=4, j=4)
+            src = raw[w, s, g][:].rearrange("p j (a t i) -> p t a j i", t=4, i=4)
+            if eng is scalar:
+                for t in range(t0, t1):
+                    eng.copy(out=dst[:, t], in_=src[:, t])
+            else:
+                eng.tensor_copy(out=dst[:, t0:t1], in_=src[:, t0:t1])
+
+        def quantize(eng, key, q0, w):
+            if key not in codes:
+                codes[key] = keep.tile([NP, W], U32, name="codes_" + "_".join(map(str, key)), align_bytes=64)
+                scales[key] = keep.tile([NP, W], U8, name="scales_" + "_".join(map(str, key)), align_bytes=64)
+            eng.quantize_mx(
+                out=codes[key][:, q0 : q0 + w].bitcast(FP8X4),
+                scales=scales[key][:, q0 : q0 + w],
+                in_=grouped[key][:, 4 * q0 : 4 * (q0 + w)],
+            )
+
+        def mx(eng, ps, lhs, m0, rhs, start, stop):
+            eng.matmul_mx(
+                out=ps[:],
+                lhsT=codes[lhs][:, m0 : m0 + NP].bitcast(FP8X4),
+                lhsT_scale=scales[lhs][:, m0 : m0 + NP],
+                rhs=codes[rhs][:].bitcast(FP8X4),
+                rhs_scale=scales[rhs][:],
+                start=start,
+                stop=stop,
+            )
+
+        def turn(eng, key, h):
+            if key[0] == "f":
+                words = raw[key][:, h, :].bitcast(F32).rearrange("p (n k) -> p n k", n=2)
+            else:
+                words = raw["s", h][:, :, KP * key[1] : KP * (key[1] + 1)].bitcast(F32)
+            bank[key, h] = new_bank()
+            for n in range(2):
+                for u in range(2):
+                    col = NP * (2 * n + u)
+                    eng.transpose(bank[key, h][:, col : col + NP], words[:, n, u:256:2], ident32[:])
+
+        def gather(eng, key, h):
+            if key not in grouped:
+                new_grouped(key)
+            words = grouped[key][:, 1024 * h : 1024 * (h + 1)].bitcast(F32)
+            if key[0] == "f":
+                dst = words.rearrange("p (r n u) -> p r n u", n=2, u=2)
+                src = bank[key, h][:].rearrange("p (n u r) -> p r n u", n=2, u=2)
+            else:
+                dst = words.rearrange("p (n r u) -> p n r u", n=2, u=2)
+                src = bank[key, h][:].rearrange("p (n u r) -> p n r u", n=2, u=2)
+            copy_on(eng, dst, src)
+
+        def trunk_mm(eng, c, g, t):
+            bank["z", c, g, t] = new_bank()
+            mx(eng, bank["z", c, g, t], ("t", 0, g), NP * t, ("f", c), True, True)
+
+        def trunk_tanh(eng, c, g, t):
+            if ("th", c, g) not in act32:
+                new_act32(("th", c, g))
+            eng.activation(
+                out=act32["th", c, g][:, t, :],
+                in_=bank["z", c, g, t][:],
+                func=ACT.Tanh,
+                bias=tanh_bias[:, g, t : t + 1],
+                scale=mode_vec[:, SLOPE + g, t : t + 1],
+            )
+
+        def branch_mm(eng, w, g, t):
+            bank[w, g, t] = new_bank()
+            for s in range(2):
+                mx(eng, bank[w, g, t], (w, s, g), NP * t, ("s", s), s == 0, s == 1)
+
+        def gate(eng, g, t):
+            if ("g", g) not in act32:
+                new_act32(("g", g))
+            eng.activation(
+                out=act32["g", g][:, t, :], in_=bank["g", g, t][:], func=ACT.Sigmoid, bias=mode_vec[:, C_GATE + g, t : t + 1]
+            )
+
+        def gate_value(eng, g, t):
+            if ("flat", g) not in grouped:
+                new_grouped(("flat", g))
+            eng.scalar_tensor_tensor(
+                out=grouped["flat", g][:, W * t : W * (t + 1)],
+                in0=bank["v", g, t][:],
+                scalar=mode_vec[:, C_VAL + g, t : t + 1],
+                in1=act32["g", g][:, t, :],
+                op0=ALU.add,
+                op1=ALU.mult,
+            )
+
+        def by_four(ap, q0, w):
+            return ap[:, :, q0 : q0 + w].rearrange("p t (m i) -> p m t i", i=4)
+
+        def words_by_four(key, q0, w):
+            return grouped[key][:, 4 * q0 : 4 * (q0 + w)].rearrange("p (m i t) -> p m t i", i=4, t=4)
+
+        def interleave_beta(eng, g):
+            new_grouped(("beta", g))
+            flat = grouped["flat", g][:].rearrange("p (t b) -> p t b", t=4)
+            copy_on(eng, words_by_four(("beta", g), 0, W), by_four(flat, 0, W))
+
+        def make_tau(eng, c, g, q0, w):
+            if ("tau", c, g) not in grouped:
+                new_grouped(("tau", c, g))
+            gain = mode_vec[:, AMP + g, :].unsqueeze(1).unsqueeze(3).broadcast_to([NP, w // 4, 4, 4])
+            eng.tensor_tensor(
+                out=words_by_four(("tau", c, g), q0, w), in0=by_four(act32["th", c, g], q0, w), in1=gain, op=ALU.mult
+            )
+
+        def field_mm(eng, n):
+            bank["o", n] = new_bank()
+            for g in range(2):
+                mx(eng, bank["o", n], ("tau", n // 4, g), NP * (n % 4), ("beta", g), g == 0, g == 1)
+
+        def impose(eng, n):
+            turned[n] = work.tile([NP, W], F32, name="turned", tag="turned", bufs=10)
+            gain, offset = dist_scaled[:, n : n + 1], query_vec[:, 16 + n : 17 + n]
+            if eng is scalar:
+                eng.activation(out=turned[n][:], in_=bank["o", n][:], func=ACT.Identity, bias=offset, scale=gain)
+            else:
+                eng.tensor_scalar(out=turned[n][:], in0=bank["o", n][:], scalar1=gain, scalar2=offset, op0=ALU.mult, op1=ALU.add)
+
+        def turn_back(eng, n0, nn, b0):
+            bank["r", n0, b0] = new_bank()
+            for k in range(4 // nn):
+                for n in range(nn):
+                    col = NP * (nn * k + n)
+                    src = turned[n0 + n][:, NP * (b0 + k) : NP * (b0 + k + 1)]
+                    eng.transpose(bank["r", n0, b0][:, col : col + NP], src, ident32[:])
+
+        def unload(eng, n0, nn, b0):
+            result[n0, b0] = work.tile([NP, W], F32, name="res", tag="res", bufs=8)
+            copy_on(eng, result[n0, b0][:], bank["r", n0, b0][:])
+
+        def store(eng, n0, nn, b0):
+            nb = 4 // nn
+            dst = out[NP * b0 : NP * (b0 + nb), NP * n0 : NP * (n0 + nn)]
+            eng.dma_start(out=dst.rearrange("(k p) q -> p k q", p=NP), in_=result[n0, b0][:].rearrange("p (k q) -> p k q", k=nb))
+
+        result = {}
+
+        def four(fn, *a):
+            return [(fn, *a, t) for t in range(4)]
+
+        def halves(fn, key):
+            return [(fn, key, h) for h in range(2)]
+
+        def lay(w, s, g):
+            return (interleave, w, s, g, 0, 4)
+
+        def quant(*key):
+            return (quantize, key, 0, W)
+
+        def tau(c, g, q0=0, w=W):
+            return (make_tau, c, g, q0, w)
+
+        def qtau(c, g, q0=0, w=W):
+            return (quantize, ("tau", c, g), q0, w)
+
+
+        def banks_of(fn, n0, nn):
+            return [(fn, n0, nn, b0) for b0 in range(0, 4, 4 // nn)]
+
+        def imposes(n0, n1):
+            return [(impose, n) for n in range(n0, n1)]
+
+        def fields(n0, n1):
+            return [(field_mm, n) for n in range(n0, n1)]
+
+        sync_order = [(load_feat, 0)] + [(load_mode_rows, row) for row in (C_TRUNK, SLOPE, AMP, C_VAL, C_GATE)]
+        sync_order += [(load_weight, "t", 0, 0), (load_feat, 1), (load_weight, "t", 0, 1), (load_query_rows, 0), (load_query_rows, 16)]
+        sync_order += [(load_weight, "g", 0, 0), (load_weight, "v", 0, 0), (load_sens, 0), (load_sens, 1), (load_weight, "g", 1, 0)]
+        sync_order += [(load_weight, "v", 1, 0), (load_feat, 2), (load_weight, "v", 0, 1), (load_feat, 3), (load_weight, "g", 1, 1)]
+        sync_order += [(load_weight, "g", 0, 1), (load_weight, "v", 1, 1)]
+        sync_order += banks_of(store, 0, 4) + banks_of(store, 4, 4) + banks_of(store, 8, 4) + banks_of(store, 12, 2) + banks_of(store, 14, 2)
+
+        pool_order = [(clear, "warm"), (identity32,), (identity16,)]
+
+        scalar_order = [(warm_up,), (order_mode_rows,)] + halves(gather, ("f", 0)) + [(gather_mode,)] + halves(gather, ("f", 1))
+        scalar_order += four(trunk_tanh, 0, 0) + four(trunk_tanh, 0, 1) + four(trunk_tanh, 1, 0)
+        scalar_order += [(gather, ("s", s), h) for s in range(2) for h in range(2)] + [lay("g", 1, 0), (gather_query,)]
+        scalar_order += four(trunk_tanh, 1, 1) + halves(gather, ("f", 2)) + four(gate, 0) + [lay("g", 0, 1)] + halves(gather, ("f", 3))
+        scalar_order += four(trunk_tanh, 2, 0) + four(gate, 1) + [(interleave_beta, 0)] + four(trunk_tanh, 2, 1)
+        scalar_order += four(trunk_tanh, 3, 0) + four(trunk_tanh, 3, 1) + imposes(0, 7)
+        scalar_order += banks_of(unload, 0, 4) + banks_of(unload, 4, 4)[:2] + imposes(8, 11) + banks_of(unload, 4, 4)[2:] + [(unload, 8, 4, 0), (unload, 8, 4, 1), (impose, 12), (unload, 8, 4, 2)]
+        scalar_order += [(unload, 12, 2, 0), (unload, 14, 2, 0)]
+
+        vector_order = [(clear, "mode"), (clear, "query"), lay("t", 0, 0), quant("f", 0), quant("t", 0, 0), (make_tanh_bias,), lay("t", 0, 1), quant("f", 1)]
+        vector_order += [quant("t", 0, 1), lay("g", 0, 0), lay("v", 0, 0), tau(0, 0), quant("g", 0, 0), qtau(0, 0), tau(0, 1), quant("v", 0, 0)]
+        vector_order += [quant("s", 0), quant("s", 1), lay("v", 1, 0), quant("g", 1, 0), quant("v", 1, 0), tau(1, 0), lay("v", 0, 1), quant("f", 2), quant("v", 0, 1)]
+        vector_order += [lay("g", 1, 1), lay("v", 1, 1), quant("g", 1, 1), quant("g", 0, 1)] + four(gate_value, 0) + [quant("f", 3), quant("v", 1, 1), tau(1, 1)]
+        vector_order += four(gate_value, 1) + [qtau(0, 1), (interleave_beta, 1), quant("beta", 0), quant("beta", 1), qtau(1, 0), qtau(1, 1)]
+        vector_order += [tau(2, 0), tau(2, 1), (impose, 7), tau(3, 0, 0, 256), qtau(2, 0), qtau(2, 1), tau(3, 1, 0, 256), qtau(3, 0, 0, 256), qtau(3, 1, 0, 256)]
+        vector_order += [(impose, 11), tau(3, 0, 256, 256), tau(3, 1, 256, 256), qtau(3, 0, 256, 256), qtau(3, 1, 256, 256)]
+        vector_order += [(impose, 13), (unload, 8, 4, 3), (impose, 14), (impose, 15), (unload, 12, 2, 2), (unload, 14, 2, 2)]
+
+        tensor_order = halves(turn, ("f", 0)) + [(turn_mode_rows,)] + halves(turn, ("f", 1)) + four(trunk_mm, 0, 0)
+        tensor_order += four(trunk_mm, 0, 1) + four(trunk_mm, 1, 0) + [(turn, ("s", s), h) for s in range(2) for h in range(2)] + [(turn_query_rows,)]
+        tensor_order += four(trunk_mm, 1, 1) + halves(turn, ("f", 2)) + four(branch_mm, "g", 0) + halves(turn, ("f", 3)) + four(branch_mm, "v", 0)
+        tensor_order += four(trunk_mm, 2, 0) + four(branch_mm, "g", 1) + four(branch_mm, "v", 1)
+        tensor_order += four(trunk_mm, 2, 1) + four(trunk_mm, 3, 0) + four(trunk_mm, 3, 1) + fields(0, 8)
+        tensor_order += banks_of(turn_back, 0, 4) + banks_of(turn_back, 4, 4) + fields(8, 14) + banks_of(turn_back, 8, 4)
+        tensor_order += fields(14, 16) + banks_of(turn_back, 12, 2) + banks_of(turn_back, 14, 2)
+
+        programs = [(gpsimd, pool_order), (sync, sync_order), (vector, vector_order), (scalar, scalar_order), (tensor, tensor_order)]
+
+
+        steps = [st for (eng, order) in programs for st in order]
+
+        def covering(fn, key, lo, hi):
+            return [st for st in steps if st[0] is fn and st[1] == key and st[2] < hi and st[2] + st[3] > lo]
+
+        def inputs(step):
+            fn, a = step[0], step[1:]
+            if fn is load_query_rows:
+                return [(clear, "query")]
+            if fn is warm_up:
+                return [(clear, "warm")]
+            if fn is order_mode_rows:
+                return [(clear, "mode")] + [st for st in steps if st[0] is load_mode_rows]
+            if fn is turn_mode_rows:
+                return [(order_mode_rows,), (identity16,)]
+            if fn is gather_mode:
+                return [(turn_mode_rows,)]
+            if fn is make_tanh_bias:
+                return [(gather_mode,)]
+            if fn is turn_query_rows:
+                return [(load_query_rows, 0), (load_query_rows, 16), (identity16,)]
+            if fn is gather_query:
+                return [(turn_query_rows,)]
+            if fn is interleave:
+                return [(load_weight, *a[:3])]
+            if fn is turn:
+                return [(identity32,), (load_feat, a[0][1]) if a[0][0] == "f" else (load_sens, a[1])]
+            if fn is gather:
+                return [(turn, *a)]
+            if fn is quantize:
+                kind = a[0][0]
+                if kind in ("f", "s"):
+                    return [(gather, a[0], 0), (gather, a[0], 1)]
+                if kind == "beta":
+                    return [(interleave_beta, a[0][1])]
+                if kind == "tau":
+                    return [(make_tau, *a[0][1:], *a[1:])]
+                return [st for st in steps if st[0] is interleave and st[1:4] == a[0]]
+            if fn is trunk_mm:
+                return covering(quantize, ("t", 0, a[1]), 0, W) + covering(quantize, ("f", a[0]), 0, W)
+            if fn is trunk_tanh:
+                return [(trunk_mm, *a), (make_tanh_bias,)]
+            if fn is branch_mm:
+                return [st for s in range(2) for key in ((a[0], s, a[1]), ("s", s)) for st in covering(quantize, key, 0, W)]
+            if fn is gate:
+                return [(branch_mm, "g", *a), (gather_mode,)]
+            if fn is gate_value:
+                return [(branch_mm, "v", *a), (gate, *a)]
+            if fn is interleave_beta:
+                return [(gate_value, a[0], t) for t in range(4)]
+            if fn is make_tau:
+                return [(trunk_tanh, a[0], a[1], t) for t in range(4)]
+            if fn is field_mm:
+                lo = NP * (a[0] % 4)
+                taus = [st for g in range(2) for st in covering(quantize, ("tau", a[0] // 4, g), lo, lo + NP)]
+                return taus + [(quantize, ("beta", g), 0, W) for g in range(2)]
+            if fn is impose:
+                return [(field_mm, *a), (gather_query,)]
+            if fn is turn_back:
+                return [(impose, a[0] + n) for n in range(a[1])]
+            if fn is unload:
+                return [(turn_back, *a)]
+            if fn is store:
+                return [(unload, *a)]
+            return []
+
+        traced, place = set(), [0] * len(programs)
+        while len(traced) < len(steps):
+            before = len(traced)
+            for e, (eng, order) in enumerate(programs):
+                if place[e] < len(order) and all(st in traced for st in inputs(order[place[e]])):
+                    step = order[place[e]]
+                    step[0](eng, *step[1:])
+                    traced.add(step)
+                    place[e] += 1
+            assert len(traced) > before

@@ -27,7 +27,8 @@ def tile_gated_deeponet_meet_f5_kernel(
     with ExitStack() as ctx:
         keep = ctx.enter_context(tc.tile_pool(name="keep", bufs=1))
         work = ctx.enter_context(tc.tile_pool(name="work", bufs=1))
-        psum = ctx.enter_context(tc.psum_pool(name="psum", bufs=8))
+        psum = ctx.enter_context(tc.psum_pool(name="psum", bufs=7))
+        psum_keep = ctx.enter_context(tc.psum_pool(name="psum_keep", bufs=1))
         ctx.enter_context(tc.manual_schedule())
 
         weights = {"t": w_trunk, "v": w_val, "g": w_gate}
@@ -43,6 +44,8 @@ def tile_gated_deeponet_meet_f5_kernel(
         tanh_bias = keep.tile([NP, 2, 4], F32, name="tanh_bias")
         query_vec = keep.tile([NP, 32], F32, name="query_vec")
         dist_scaled = keep.tile([NP, 16], F32, name="dist_scaled")
+        ones = keep.tile([NP, 16], F32, name="ones")
+        amp_late = keep.tile([NP, 16, 4], F32, name="amp_late")
         warm = keep.tile([NP, 8], F32, name="warm")
         warm_out = keep.tile([NP, 8], F32, name="warm_out")
         C_TRUNK, SLOPE, AMP, C_VAL, C_GATE = 0, 2, 4, 6, 8
@@ -51,7 +54,7 @@ def tile_gated_deeponet_meet_f5_kernel(
             return psum.tile([NP, W if dtype == F32 else 2 * W], dtype, name="bank", tag="bank")
 
         def new_grouped(key):
-            grouped[key] = work.tile([NP, 4 * W], BF16, name="grouped", tag="grouped", bufs=6, align_bytes=64)
+            grouped[key] = work.tile([NP, 4 * W], BF16, name="grouped", tag="grouped", bufs=7, align_bytes=64)
             return grouped[key]
 
         def new_act32(key):
@@ -59,17 +62,18 @@ def tile_gated_deeponet_meet_f5_kernel(
             return act32[key]
 
         def load_weight(eng, w, s, g):
-            raw[w, s, g] = work.tile([NP, 4, W], BF16, name="raw", tag="raw", bufs=9)
+            raw[w, s, g] = work.tile([NP, 4, W], BF16, name="raw", tag="raw", bufs=10)
             src = weights[w][KP * s : KP * (s + 1), W * g : W * (g + 1)]
             eng.dma_start(out=raw[w, s, g][:], in_=src.rearrange("(p j) c -> p j c", j=4))
 
-        def load_feat(eng, c):
-            raw["f", c] = work.tile([NP, 2, 2 * KP], BF16, name="raw", tag="raw", bufs=9)
-            src = feat[W * c : W * (c + 1), :]
-            eng.dma_start(out=raw["f", c][:], in_=src.rearrange("(h p n) k -> p h (n k)", h=2, n=2))
+        def load_feat(eng, c, h0, nh):
+            if ("f", c) not in raw:
+                raw["f", c] = work.tile([NP, 2, 2 * KP], BF16, name="raw", tag="raw", bufs=10)
+            src = feat[W * c + 256 * h0 : W * c + 256 * (h0 + nh), :]
+            eng.dma_start(out=raw["f", c][:, h0 : h0 + nh, :], in_=src.rearrange("(h p n) k -> p h (n k)", h=nh, n=2))
 
         def load_sens(eng, h):
-            raw["s", h] = work.tile([NP, 2, S], BF16, name="raw", tag="raw", bufs=9)
+            raw["s", h] = work.tile([NP, 2, S], BF16, name="raw", tag="raw", bufs=10)
             src = sens[256 * h : 256 * (h + 1), :]
             eng.dma_start(out=raw["s", h][:], in_=src.rearrange("(n p) k -> p n k", p=NP))
 
@@ -104,7 +108,7 @@ def tile_gated_deeponet_meet_f5_kernel(
             copy_on(eng, dst, mode_rows[0:10, :].rearrange("r (a t i) -> r t a i", t=4, i=4))
 
         def turn_mode_rows(eng):
-            bank["mode"] = new_bank(BF16)
+            bank["mode"] = psum_keep.tile([NP, 2 * W], BF16, name="mode_bank")
             for t in range(4):
                 cols = slice(NP * t, NP * (t + 1))
                 eng.transpose(bank["mode"][:, cols], mode_rows_t[:, cols], ident16[:])
@@ -125,7 +129,8 @@ def tile_gated_deeponet_meet_f5_kernel(
             eng.activation(out=dist_scaled[:], in_=bank["query"][:, 0:16], func=ACT.Copy, scale=1.0 / 32.0)
             eng.copy(out=query_vec[:, 16:32], in_=bank["query"][:, 16:32])
 
-        def interleave(eng, w, s, g, t0, t1):
+        def interleave(eng, w, s, g, t0, nt):
+            t1 = t0 + nt
             if (w, s, g) not in grouped:
                 new_grouped((w, s, g))
             dst = grouped[w, s, g][:].rearrange("p (t a i j) -> p t a j i", t=4, i=4, j=4)
@@ -135,6 +140,31 @@ def tile_gated_deeponet_meet_f5_kernel(
                     eng.copy(out=dst[:, t], in_=src[:, t])
             else:
                 eng.tensor_copy(out=dst[:, t0:t1], in_=src[:, t0:t1])
+
+        def release(eng, k):
+            eng.memset(ones[:, k : k + 1], 1.0)
+
+        def release_amp(eng, k, g):
+            eng.tensor_copy(out=amp_late[:, k, :], in_=bank["mode"][:, AMP + g : W : NP])
+
+        def pool_interleave(eng, key, t, k):
+            if key not in grouped:
+                new_grouped(key)
+            if key[0] == "beta":
+                src = grouped["flat", key[1]][:].rearrange("p (t m b) -> p m b t", t=4, m=4)[:, t]
+                dst = grouped[key][:, W * t : W * (t + 1)].rearrange("p (b t) -> p b t", t=4)
+            else:
+                src = raw[key][:].rearrange("p j (a t i) -> p t a i j", t=4, i=4)[:, t]
+                dst = grouped[key][:, W * t : W * (t + 1)].rearrange("p (a i j) -> p a i j", i=4, j=4)
+            eng.tensor_scalar(out=dst, in0=src, scalar1=ones[:, k : k + 1], scalar2=0.0, op0=ALU.mult, op1=ALU.add)
+
+        def pool_tau(eng, c, g, q0, w, k):
+            if ("tau", c, g) not in grouped:
+                new_grouped(("tau", c, g))
+            dst = grouped["tau", c, g][:, 4 * q0 : 4 * (q0 + w)].rearrange("p (q t) -> p q t", t=4)
+            src = act32["th", c, g][:, :, q0 : q0 + w].rearrange("p t q -> p q t")
+            gain = amp_late[:, k, :].unsqueeze(1).broadcast_to([NP, w, 4])
+            eng.tensor_tensor(out=dst, in0=src, in1=gain, op=ALU.mult)
 
         def quantize(eng, key, q0, w):
             if key not in codes:
@@ -146,13 +176,13 @@ def tile_gated_deeponet_meet_f5_kernel(
                 in_=grouped[key][:, 4 * q0 : 4 * (q0 + w)],
             )
 
-        def mx(eng, ps, lhs, m0, rhs, start, stop):
+        def mx(eng, ps, lhs, m0, rhs, lo, w, start, stop):
             eng.matmul_mx(
-                out=ps[:],
+                out=ps[:, 0:w],
                 lhsT=codes[lhs][:, m0 : m0 + NP].bitcast(FP8X4),
                 lhsT_scale=scales[lhs][:, m0 : m0 + NP],
-                rhs=codes[rhs][:].bitcast(FP8X4),
-                rhs_scale=scales[rhs][:],
+                rhs=codes[rhs][:, lo : lo + w].bitcast(FP8X4),
+                rhs_scale=scales[rhs][:, lo : lo + w],
                 start=start,
                 stop=stop,
             )
@@ -180,16 +210,16 @@ def tile_gated_deeponet_meet_f5_kernel(
                 src = bank[key, h][:].rearrange("p (n u r) -> p n r u", n=2, u=2)
             copy_on(eng, dst, src)
 
-        def trunk_mm(eng, c, g, t):
-            bank["z", c, g, t] = new_bank()
-            mx(eng, bank["z", c, g, t], ("t", 0, g), NP * t, ("f", c), True, True)
+        def trunk_mm(eng, c, g, lo, w, t):
+            bank["z", c, g, lo, t] = new_bank()
+            mx(eng, bank["z", c, g, lo, t], ("t", 0, g), NP * t, ("f", c), lo, w, True, True)
 
-        def trunk_tanh(eng, c, g, t):
+        def trunk_tanh(eng, c, g, lo, w, t):
             if ("th", c, g) not in act32:
                 new_act32(("th", c, g))
             eng.activation(
-                out=act32["th", c, g][:, t, :],
-                in_=bank["z", c, g, t][:],
+                out=act32["th", c, g][:, t, lo : lo + w],
+                in_=bank["z", c, g, lo, t][:, 0:w],
                 func=ACT.Tanh,
                 bias=tanh_bias[:, g, t : t + 1],
                 scale=mode_vec[:, SLOPE + g, t : t + 1],
@@ -198,7 +228,7 @@ def tile_gated_deeponet_meet_f5_kernel(
         def branch_mm(eng, w, g, t):
             bank[w, g, t] = new_bank()
             for s in range(2):
-                mx(eng, bank[w, g, t], (w, s, g), NP * t, ("s", s), s == 0, s == 1)
+                mx(eng, bank[w, g, t], (w, s, g), NP * t, ("s", s), 0, W, s == 0, s == 1)
 
         def gate(eng, g, t):
             if ("g", g) not in act32:
@@ -225,48 +255,50 @@ def tile_gated_deeponet_meet_f5_kernel(
         def words_by_four(key, q0, w):
             return grouped[key][:, 4 * q0 : 4 * (q0 + w)].rearrange("p (m i t) -> p m t i", i=4, t=4)
 
-        def interleave_beta(eng, g):
-            new_grouped(("beta", g))
+        def interleave_beta_part(eng, g, m0, nm):
+            if ("beta", g) not in grouped:
+                new_grouped(("beta", g))
             flat = grouped["flat", g][:].rearrange("p (t b) -> p t b", t=4)
-            copy_on(eng, words_by_four(("beta", g), 0, W), by_four(flat, 0, W))
+            copy_on(eng, words_by_four(("beta", g), NP * m0, NP * nm), by_four(flat, NP * m0, NP * nm))
 
         def make_tau(eng, c, g, q0, w):
             if ("tau", c, g) not in grouped:
                 new_grouped(("tau", c, g))
-            gain = mode_vec[:, AMP + g, :].unsqueeze(1).unsqueeze(3).broadcast_to([NP, w // 4, 4, 4])
+            gain = bank["mode"][:, AMP + g : W : NP].unsqueeze(1).unsqueeze(3).broadcast_to([NP, w // 4, 4, 4])
             eng.tensor_tensor(
                 out=words_by_four(("tau", c, g), q0, w), in0=by_four(act32["th", c, g], q0, w), in1=gain, op=ALU.mult
             )
 
-        def field_mm(eng, n):
-            bank["o", n] = new_bank()
+        def field_mm(eng, n, lo, w):
+            bank["o", n, lo] = new_bank()
             for g in range(2):
-                mx(eng, bank["o", n], ("tau", n // 4, g), NP * (n % 4), ("beta", g), g == 0, g == 1)
+                mx(eng, bank["o", n, lo], ("tau", n // 4, g), NP * (n % 4), ("beta", g), lo, w, g == 0, g == 1)
 
-        def impose(eng, n):
-            turned[n] = work.tile([NP, W], F32, name="turned", tag="turned", bufs=10)
+        def impose(eng, n, lo, w):
+            if n not in turned:
+                turned[n] = work.tile([NP, W], F32, name="turned", tag="turned", bufs=8)
+            dst, src = turned[n][:, lo : lo + w], bank["o", n, lo][:, 0:w]
             gain, offset = dist_scaled[:, n : n + 1], query_vec[:, 16 + n : 17 + n]
             if eng is scalar:
-                eng.activation(out=turned[n][:], in_=bank["o", n][:], func=ACT.Identity, bias=offset, scale=gain)
+                eng.activation(out=dst, in_=src, func=ACT.Identity, bias=offset, scale=gain)
             else:
-                eng.tensor_scalar(out=turned[n][:], in0=bank["o", n][:], scalar1=gain, scalar2=offset, op0=ALU.mult, op1=ALU.add)
+                eng.tensor_scalar(out=dst, in0=src, scalar1=gain, scalar2=offset, op0=ALU.mult, op1=ALU.add)
 
-        def turn_back(eng, n0, nn, b0):
+        def turn_back(eng, n0, nn, b0, nb):
             bank["r", n0, b0] = new_bank()
-            for k in range(4 // nn):
+            for k in range(nb):
                 for n in range(nn):
                     col = NP * (nn * k + n)
                     src = turned[n0 + n][:, NP * (b0 + k) : NP * (b0 + k + 1)]
                     eng.transpose(bank["r", n0, b0][:, col : col + NP], src, ident32[:])
 
-        def unload(eng, n0, nn, b0):
-            result[n0, b0] = work.tile([NP, W], F32, name="res", tag="res", bufs=8)
-            copy_on(eng, result[n0, b0][:], bank["r", n0, b0][:])
+        def unload(eng, n0, nn, b0, nb):
+            result[n0, b0] = work.tile([NP, W], F32, name="res", tag="res", bufs=9)
+            copy_on(eng, result[n0, b0][:, 0 : NP * nn * nb], bank["r", n0, b0][:, 0 : NP * nn * nb])
 
-        def store(eng, n0, nn, b0):
-            nb = 4 // nn
-            dst = out[NP * b0 : NP * (b0 + nb), NP * n0 : NP * (n0 + nn)]
-            eng.dma_start(out=dst.rearrange("(k p) q -> p k q", p=NP), in_=result[n0, b0][:].rearrange("p (k q) -> p k q", k=nb))
+        def store(eng, n0, nn, b0, nb):
+            dst = out[NP * b0 : NP * (b0 + nb), NP * n0 : NP * (n0 + nn)].rearrange("(k p) q -> p k q", p=NP)
+            eng.dma_start(out=dst, in_=result[n0, b0][:, 0 : NP * nn * nb].rearrange("p (k q) -> p k q", k=nb))
 
         result = {}
 
@@ -290,48 +322,66 @@ def tile_gated_deeponet_meet_f5_kernel(
 
 
         def banks_of(fn, n0, nn):
-            return [(fn, n0, nn, b0) for b0 in range(0, 4, 4 // nn)]
+            return [(fn, n0, nn, b0, 4 // nn) for b0 in range(0, 4, 4 // nn)]
 
         def imposes(n0, n1):
-            return [(impose, n) for n in range(n0, n1)]
+            return [(impose, n, 0, W) for n in range(n0, n1)]
 
         def fields(n0, n1):
-            return [(field_mm, n) for n in range(n0, n1)]
+            return [(field_mm, n, 0, W) for n in range(n0, n1)]
 
-        sync_order = [(load_feat, 0)] + [(load_mode_rows, row) for row in (C_TRUNK, SLOPE, AMP, C_VAL, C_GATE)]
-        sync_order += [(load_weight, "t", 0, 0), (load_feat, 1), (load_weight, "t", 0, 1), (load_query_rows, 0), (load_query_rows, 16)]
-        sync_order += [(load_weight, "g", 0, 0), (load_weight, "v", 0, 0), (load_sens, 0), (load_sens, 1), (load_weight, "g", 1, 0)]
-        sync_order += [(load_weight, "v", 1, 0), (load_feat, 2), (load_weight, "v", 0, 1), (load_feat, 3), (load_weight, "g", 1, 1)]
-        sync_order += [(load_weight, "g", 0, 1), (load_weight, "v", 1, 1)]
-        sync_order += banks_of(store, 0, 4) + banks_of(store, 4, 4) + banks_of(store, 8, 4) + banks_of(store, 12, 2) + banks_of(store, 14, 2)
+        def tanhs(c, g, lo=0, w=W):
+            return four(trunk_tanh, c, g, lo, w)
+
+        def zs(c, g, lo=0, w=W):
+            return four(trunk_mm, c, g, lo, w)
+
+        def pooled(key, k, ts=range(4)):
+            return [(pool_interleave, key, t, k) for t in ts]
+
+        def part(w, s, g, t0, nt):
+            return (interleave, w, s, g, t0, nt)
+
+        def qpart(key, lo, w):
+            return (quantize, key, lo, w)
+
+        sync_order = [(load_feat, 0, 0, 1)] + [(load_mode_rows, row) for row in (C_TRUNK, SLOPE, AMP, C_VAL, C_GATE)]
+        sync_order += [(load_weight, "t", 0, 0), (load_feat, 0, 1, 1), (load_weight, "t", 0, 1), (load_query_rows, 0), (load_query_rows, 16)]
+        sync_order += [(load_weight, "g", 0, 0), (load_weight, "g", 1, 0), (load_sens, 0), (load_feat, 1, 0, 2), (load_weight, "v", 0, 0), (load_sens, 1)]
+        sync_order += [(load_weight, "v", 1, 0), (load_weight, "g", 0, 1), (load_feat, 2, 0, 2), (load_weight, "g", 1, 1), (load_weight, "v", 1, 1)]
+        sync_order += [(load_weight, "v", 0, 1), (load_feat, 3, 0, 2)]
+        sync_order += banks_of(store, 0, 4) + banks_of(store, 4, 4) + banks_of(store, 8, 4) + banks_of(store, 12, 2) + [(store, 14, 2, b0, 1) for b0 in range(4)]
 
         pool_order = [(clear, "warm"), (identity32,), (identity16,)]
+        pool_order += pooled(("g", 1, 0), 0) + pooled(("v", 0, 0), 0, [0]) + pooled(("g", 1, 1), 1, [0, 1]) + pooled(("v", 1, 1), 2) + pooled(("beta", 0), 3, [0, 1])
+        pool_order += [(pool_tau, 1, 1, 0, 256, 0), (pool_tau, 2, 1, 0, 256, 1), (pool_tau, 3, 1, 0, 256, 2)]
 
-        scalar_order = [(warm_up,), (order_mode_rows,)] + halves(gather, ("f", 0)) + [(gather_mode,)] + halves(gather, ("f", 1))
-        scalar_order += four(trunk_tanh, 0, 0) + four(trunk_tanh, 0, 1) + four(trunk_tanh, 1, 0)
-        scalar_order += [(gather, ("s", s), h) for s in range(2) for h in range(2)] + [lay("g", 1, 0), (gather_query,)]
-        scalar_order += four(trunk_tanh, 1, 1) + halves(gather, ("f", 2)) + four(gate, 0) + [lay("g", 0, 1)] + halves(gather, ("f", 3))
-        scalar_order += four(trunk_tanh, 2, 0) + four(gate, 1) + [(interleave_beta, 0)] + four(trunk_tanh, 2, 1)
-        scalar_order += four(trunk_tanh, 3, 0) + four(trunk_tanh, 3, 1) + imposes(0, 7)
-        scalar_order += banks_of(unload, 0, 4) + banks_of(unload, 4, 4)[:2] + imposes(8, 11) + banks_of(unload, 4, 4)[2:] + [(unload, 8, 4, 0), (unload, 8, 4, 1), (impose, 12), (unload, 8, 4, 2)]
-        scalar_order += [(unload, 12, 2, 0), (unload, 14, 2, 0)]
+        scalar_order = [(warm_up,), (order_mode_rows,), part("t", 0, 0, 0, 2), (gather_mode,), (gather, ("f", 0), 1), part("t", 0, 1, 0, 2)]
+        scalar_order += tanhs(0, 0, 0, 256) + tanhs(0, 0, 256, 256) + tanhs(0, 1) + halves(gather, ("f", 1)) + [part("v", 0, 0, 1, 3)]
+        scalar_order += [(gather, ("s", 0), 1)] + halves(gather, ("s", 1)) + tanhs(1, 0) + halves(gather, ("f", 2)) + [(gather_query,)] + tanhs(1, 1)
+        scalar_order += [part("g", 1, 1, 2, 2)] + four(gate, 0) + [lay("v", 0, 1)] + tanhs(2, 0)[:2] + [(gather, ("f", 3), 1)] + four(gate, 1)
+        scalar_order += [(interleave_beta_part, 0, 2, 2)] + tanhs(2, 0)[2:] + tanhs(2, 1) + tanhs(3, 1)[:2] + imposes(0, 2) + tanhs(3, 1)[2:] + tanhs(3, 0)
+        scalar_order += imposes(7, 8) + banks_of(unload, 0, 4) + imposes(8, 11) + banks_of(unload, 4, 4)[:3] + banks_of(unload, 8, 4)[:1]
+        scalar_order += imposes(12, 15) + [(unload, 8, 4, 3, 1), (unload, 12, 2, 2, 2), (unload, 14, 2, 0, 1), (unload, 14, 2, 2, 1)]
 
-        vector_order = [(clear, "mode"), (clear, "query"), lay("t", 0, 0), quant("f", 0), quant("t", 0, 0), (make_tanh_bias,), lay("t", 0, 1), quant("f", 1)]
-        vector_order += [quant("t", 0, 1), lay("g", 0, 0), lay("v", 0, 0), tau(0, 0), quant("g", 0, 0), qtau(0, 0), tau(0, 1), quant("v", 0, 0)]
-        vector_order += [quant("s", 0), quant("s", 1), lay("v", 1, 0), quant("g", 1, 0), quant("v", 1, 0), tau(1, 0), lay("v", 0, 1), quant("f", 2), quant("v", 0, 1)]
-        vector_order += [lay("g", 1, 1), lay("v", 1, 1), quant("g", 1, 1), quant("g", 0, 1)] + four(gate_value, 0) + [quant("f", 3), quant("v", 1, 1), tau(1, 1)]
-        vector_order += four(gate_value, 1) + [qtau(0, 1), (interleave_beta, 1), quant("beta", 0), quant("beta", 1), qtau(1, 0), qtau(1, 1)]
-        vector_order += [tau(2, 0), tau(2, 1), (impose, 7), tau(3, 0, 0, 256), qtau(2, 0), qtau(2, 1), tau(3, 1, 0, 256), qtau(3, 0, 0, 256), qtau(3, 1, 0, 256)]
-        vector_order += [(impose, 11), tau(3, 0, 256, 256), tau(3, 1, 256, 256), qtau(3, 0, 256, 256), qtau(3, 1, 256, 256)]
-        vector_order += [(impose, 13), (unload, 8, 4, 3), (impose, 14), (impose, 15), (unload, 12, 2, 2), (unload, 14, 2, 2)]
+        vector_order = [(clear, "mode"), (clear, "query"), (gather, ("f", 0), 0), qpart(("f", 0), 0, 256), part("t", 0, 0, 2, 2), qpart(("t", 0, 0), 0, 256), (make_tanh_bias,)]
+        vector_order += [qpart(("t", 0, 0), 256, 256), part("t", 0, 1, 2, 2), qpart(("f", 0), 256, 256), lay("g", 0, 0), quant("t", 0, 1), quant("g", 0, 0)]
+        vector_order += [(release, 0), tau(0, 0), (gather, ("s", 0), 0), tau(0, 1), quant("f", 1), lay("v", 1, 0), quant("s", 0), quant("g", 1, 0), quant("s", 1)]
+        vector_order += [lay("g", 0, 1), quant("v", 1, 0), quant("v", 0, 0), quant("g", 0, 1), (release, 1), tau(1, 0), qtau(0, 0), quant("g", 1, 1), quant("f", 2)]
+        vector_order += [(release, 2)] + four(gate_value, 0) + [tau(1, 1, 256, 256), (gather, ("f", 3), 0), quant("v", 0, 1), quant("v", 1, 1), quant("f", 3), qtau(1, 0)]
+        vector_order += [(release, 3)] + four(gate_value, 1) + [qtau(0, 1), (interleave_beta_part, 1, 0, 4), quant("beta", 0), quant("beta", 1)]
+        vector_order += [(release_amp, 0, 1), tau(2, 0)] + imposes(2, 3) + [qtau(2, 0), qtau(1, 1)]
+        vector_order += [(release_amp, 1, 1), tau(2, 1, 256, 256)] + imposes(3, 7) + [qtau(2, 1)]
+        vector_order += [(release_amp, 2, 1), tau(3, 1, 256, 256), tau(3, 0)] + imposes(11, 12) + [qtau(3, 0), qtau(3, 1)]
+        vector_order += [(unload, 4, 4, 3, 1), (unload, 8, 4, 1, 1), (unload, 8, 4, 2, 1)] + imposes(15, 16) + [(unload, 12, 2, 0, 2), (unload, 14, 2, 1, 1), (unload, 14, 2, 3, 1)]
 
-        tensor_order = halves(turn, ("f", 0)) + [(turn_mode_rows,)] + halves(turn, ("f", 1)) + four(trunk_mm, 0, 0)
-        tensor_order += four(trunk_mm, 0, 1) + four(trunk_mm, 1, 0) + [(turn, ("s", s), h) for s in range(2) for h in range(2)] + [(turn_query_rows,)]
-        tensor_order += four(trunk_mm, 1, 1) + halves(turn, ("f", 2)) + four(branch_mm, "g", 0) + halves(turn, ("f", 3)) + four(branch_mm, "v", 0)
-        tensor_order += four(trunk_mm, 2, 0) + four(branch_mm, "g", 1) + four(branch_mm, "v", 1)
-        tensor_order += four(trunk_mm, 2, 1) + four(trunk_mm, 3, 0) + four(trunk_mm, 3, 1) + fields(0, 8)
-        tensor_order += banks_of(turn_back, 0, 4) + banks_of(turn_back, 4, 4) + fields(8, 14) + banks_of(turn_back, 8, 4)
-        tensor_order += fields(14, 16) + banks_of(turn_back, 12, 2) + banks_of(turn_back, 14, 2)
+        tensor_order = [(turn, ("f", 0), 0), (turn_mode_rows,), (turn, ("f", 0), 1)] + zs(0, 0, 0, 256) + [(turn_query_rows,)] + zs(0, 0, 256, 256)
+        tensor_order += zs(0, 1) + [(turn, ("s", 0), 0)] + halves(turn, ("f", 1)) + [(turn, ("s", 0), 1)] + halves(turn, ("s", 1)) + zs(1, 0)
+        tensor_order += halves(turn, ("f", 2)) + zs(1, 1) + four(branch_mm, "g", 0) + four(branch_mm, "v", 0) + four(branch_mm, "g", 1)[:2]
+        tensor_order += halves(turn, ("f", 3)) + zs(2, 0)[:2] + four(branch_mm, "g", 1)[2:] + four(branch_mm, "v", 1) + zs(2, 0)[2:] + zs(2, 1) + zs(3, 1)[:2]
+        tensor_order += fields(0, 4) + zs(3, 1)[2:] + zs(3, 0) + fields(4, 8) + banks_of(turn_back, 0, 4) + fields(8, 12)
+        tensor_order += banks_of(turn_back, 4, 4) + banks_of(turn_back, 8, 4)[:3] + fields(12, 16) + banks_of(turn_back, 8, 4)[3:]
+        tensor_order += banks_of(turn_back, 12, 2) + [(turn_back, 14, 2, b0, 1) for b0 in range(4)]
 
         programs = [(gpsimd, pool_order), (sync, sync_order), (vector, vector_order), (scalar, scalar_order), (tensor, tensor_order)]
 
@@ -339,7 +389,8 @@ def tile_gated_deeponet_meet_f5_kernel(
         steps = [st for (eng, order) in programs for st in order]
 
         def covering(fn, key, lo, hi):
-            return [st for st in steps if st[0] is fn and st[1] == key and st[2] < hi and st[2] + st[3] > lo]
+            n = len(key) + 1
+            return [st for st in steps if st[0] is fn and st[1:n] == key and st[n] < hi and st[n] + st[n + 1] > lo]
 
         def inputs(step):
             fn, a = step[0], step[1:]
@@ -361,41 +412,51 @@ def tile_gated_deeponet_meet_f5_kernel(
                 return [(turn_query_rows,)]
             if fn is interleave:
                 return [(load_weight, *a[:3])]
+            if fn is release_amp:
+                return [(gather_mode,)]
+            if fn is pool_interleave:
+                return [(release, a[2])] + ([(gate_value, a[0][1], t) for t in range(4)] if a[0][0] == "beta" else [(load_weight, *a[0])])
+            if fn is pool_tau:
+                return [(release_amp, a[4], a[1])] + covering(trunk_tanh, a[:2], a[2], a[2] + a[3])
             if fn is turn:
-                return [(identity32,), (load_feat, a[0][1]) if a[0][0] == "f" else (load_sens, a[1])]
+                loads = covering(load_feat, a[0][1:], a[1], a[1] + 1) if a[0][0] == "f" else [(load_sens, a[1])]
+                return [(identity32,)] + loads
             if fn is gather:
                 return [(turn, *a)]
             if fn is quantize:
-                kind = a[0][0]
-                if kind in ("f", "s"):
-                    return [(gather, a[0], 0), (gather, a[0], 1)]
-                if kind == "beta":
-                    return [(interleave_beta, a[0][1])]
-                if kind == "tau":
-                    return [(make_tau, *a[0][1:], *a[1:])]
-                return [st for st in steps if st[0] is interleave and st[1:4] == a[0]]
+                key, lo, hi = a[0], a[1], a[1] + a[2]
+                if key[0] in ("f", "s"):
+                    return [(gather, key, h) for h in range(lo // 256, hi // 256)]
+                pooled = [st for st in steps if st[0] is pool_interleave and st[1] == key and lo <= NP * st[2] < hi]
+                if key[0] == "beta":
+                    return pooled + covering(interleave_beta_part, key[1:], 0, 4)
+                if key[0] == "tau":
+                    return covering(make_tau, key[1:], lo, hi) + covering(pool_tau, key[1:], lo, hi)
+                return pooled + covering(interleave, key, lo // NP, hi // NP)
             if fn is trunk_mm:
-                return covering(quantize, ("t", 0, a[1]), 0, W) + covering(quantize, ("f", a[0]), 0, W)
+                c, g, lo, w, t = a
+                return covering(quantize, (("t", 0, g),), NP * t, NP * t + NP) + covering(quantize, (("f", c),), lo, lo + w)
             if fn is trunk_tanh:
                 return [(trunk_mm, *a), (make_tanh_bias,)]
             if fn is branch_mm:
-                return [st for s in range(2) for key in ((a[0], s, a[1]), ("s", s)) for st in covering(quantize, key, 0, W)]
+                return [st for s in range(2) for key in ((a[0], s, a[1]), ("s", s)) for st in covering(quantize, (key,), 0, W)]
             if fn is gate:
                 return [(branch_mm, "g", *a), (gather_mode,)]
             if fn is gate_value:
                 return [(branch_mm, "v", *a), (gate, *a)]
-            if fn is interleave_beta:
+            if fn is interleave_beta_part:
                 return [(gate_value, a[0], t) for t in range(4)]
             if fn is make_tau:
-                return [(trunk_tanh, a[0], a[1], t) for t in range(4)]
+                return [(gather_mode,)] + covering(trunk_tanh, a[:2], a[2], a[2] + a[3])
             if fn is field_mm:
                 lo = NP * (a[0] % 4)
-                taus = [st for g in range(2) for st in covering(quantize, ("tau", a[0] // 4, g), lo, lo + NP)]
+                taus = [st for g in range(2) for st in covering(quantize, (("tau", a[0] // 4, g),), lo, lo + NP)]
                 return taus + [(quantize, ("beta", g), 0, W) for g in range(2)]
             if fn is impose:
                 return [(field_mm, *a), (gather_query,)]
             if fn is turn_back:
-                return [(impose, a[0] + n) for n in range(a[1])]
+                n0, nn, b0, nb = a
+                return [st for n in range(n0, n0 + nn) for st in covering(impose, (n,), NP * b0, NP * (b0 + nb))]
             if fn is unload:
                 return [(turn_back, *a)]
             if fn is store:

@@ -15,8 +15,16 @@ ACT = mybir.ActivationFunctionType
 ALU = mybir.AluOpType
 
 NP = 128
-KP = 512
 W = 512
+HALF = W // 2
+INV_SQRT_P = 1.0 / 32.0
+
+C_TRUNK, SLOPE, AMP, C_VAL, C_GATE = 0, 2, 4, 6, 8
+MODE_ROWS = 10
+TILES = Q // NP
+DIST, LIFT = 0, TILES
+
+RAW_BUFS, ROWS_BUFS, ACT_BUFS, TURNED_BUFS, RESULT_BUFS, PSUM_BANKS = 10, 7, 8, 8, 9, 7
 
 
 def tile_gated_deeponet_meet_f5_kernel(
@@ -27,55 +35,65 @@ def tile_gated_deeponet_meet_f5_kernel(
     with ExitStack() as ctx:
         keep = ctx.enter_context(tc.tile_pool(name="keep", bufs=1))
         work = ctx.enter_context(tc.tile_pool(name="work", bufs=1))
-        psum = ctx.enter_context(tc.psum_pool(name="psum", bufs=7))
+        psum = ctx.enter_context(tc.psum_pool(name="psum", bufs=PSUM_BANKS))
         psum_keep = ctx.enter_context(tc.psum_pool(name="psum_keep", bufs=1))
         ctx.enter_context(tc.manual_schedule())
 
-        weights = {"t": w_trunk, "v": w_val, "g": w_gate}
-        raw, grouped, codes, scales = {}, {}, {}, {}
-        act32, bank, turned = {}, {}, {}
+        weights = {"trunk": w_trunk, "val": w_val, "gate": w_gate}
+        raw, rows, codes, scales = {}, {}, {}, {}
+        act32, bank, turned, result = {}, {}, {}, {}
 
         ident32 = keep.tile([NP, NP], F32, name="ident32")
         ident16 = keep.tile([NP, NP], BF16, name="ident16")
-        mode_rows = keep.tile([NP, KP], BF16, name="mode_rows")
-        mode_rows_t = keep.tile([NP, KP], BF16, name="mode_rows_t")
+        mode_rows = keep.tile([NP, W], BF16, name="mode_rows")
+        mode_rows_t = keep.tile([NP, W], BF16, name="mode_rows_t")
         query_rows = keep.tile([NP, NP], BF16, name="query_rows")
-        mode_vec = keep.tile([NP, 16, 4], F32, name="mode_vec")
+        mode_vec = keep.tile([NP, MODE_ROWS, 4], F32, name="mode_vec")
         tanh_bias = keep.tile([NP, 2, 4], F32, name="tanh_bias")
-        query_vec = keep.tile([NP, 32], F32, name="query_vec")
-        dist_scaled = keep.tile([NP, 16], F32, name="dist_scaled")
-        ones = keep.tile([NP, 16], F32, name="ones")
-        amp_late = keep.tile([NP, 16, 4], F32, name="amp_late")
+        lift_vec = keep.tile([NP, TILES], F32, name="lift_vec")
+        dist_vec = keep.tile([NP, TILES], F32, name="dist_vec")
+        ones = keep.tile([NP, 4], F32, name="ones")
+        amp_copies = keep.tile([NP, 4, 4], F32, name="amp_copies")
         warm = keep.tile([NP, 8], F32, name="warm")
         warm_out = keep.tile([NP, 8], F32, name="warm_out")
-        C_TRUNK, SLOPE, AMP, C_VAL, C_GATE = 0, 2, 4, 6, 8
 
-        def new_bank(dtype=F32):
-            return psum.tile([NP, W if dtype == F32 else 2 * W], dtype, name="bank", tag="bank")
+        def new_bank():
+            return psum.tile([NP, W], F32, name="bank", tag="bank")
 
-        def new_grouped(key):
-            grouped[key] = work.tile([NP, 4 * W], BF16, name="grouped", tag="grouped", bufs=7, align_bytes=64)
-            return grouped[key]
+        def raw_tile(key, shape):
+            if key not in raw:
+                raw[key] = work.tile(shape, BF16, name="raw", tag="raw", bufs=RAW_BUFS)
+            return raw[key]
 
-        def new_act32(key):
-            act32[key] = work.tile([NP, 4, W], F32, name="act32", tag="act32", bufs=8)
+        def rows_tile(key):
+            if key not in rows:
+                rows[key] = work.tile([NP, 4 * W], BF16, name="rows", tag="rows", bufs=ROWS_BUFS, align_bytes=64)
+            return rows[key]
+
+        def act_tile(key):
+            if key not in act32:
+                act32[key] = work.tile([NP, 4, W], F32, name="act32", tag="act32", bufs=ACT_BUFS)
             return act32[key]
 
-        def load_weight(eng, w, s, g):
-            raw[w, s, g] = work.tile([NP, 4, W], BF16, name="raw", tag="raw", bufs=10)
-            src = weights[w][KP * s : KP * (s + 1), W * g : W * (g + 1)]
-            eng.dma_start(out=raw[w, s, g][:], in_=src.rearrange("(p j) c -> p j c", j=4))
+        def copy_on(eng, dst, src):
+            if eng is scalar:
+                eng.copy(out=dst, in_=src)
+            else:
+                eng.tensor_copy(out=dst, in_=src)
+
+
+        def load_weight(eng, name, s, g):
+            src = weights[name][W * s : W * (s + 1), W * g : W * (g + 1)]
+            eng.dma_start(out=raw_tile((name, s, g), [NP, 4, W])[:], in_=src.rearrange("(p j) c -> p j c", j=4))
 
         def load_feat(eng, c, h0, nh):
-            if ("f", c) not in raw:
-                raw["f", c] = work.tile([NP, 2, 2 * KP], BF16, name="raw", tag="raw", bufs=10)
-            src = feat[W * c + 256 * h0 : W * c + 256 * (h0 + nh), :]
-            eng.dma_start(out=raw["f", c][:, h0 : h0 + nh, :], in_=src.rearrange("(h p n) k -> p h (n k)", h=nh, n=2))
+            src = feat[W * c + HALF * h0 : W * c + HALF * (h0 + nh), :]
+            dst = raw_tile(("feat", c), [NP, 2, 2 * C])[:, h0 : h0 + nh, :]
+            eng.dma_start(out=dst, in_=src.rearrange("(h p n) k -> p h (n k)", h=nh, n=2))
 
         def load_sens(eng, h):
-            raw["s", h] = work.tile([NP, 2, S], BF16, name="raw", tag="raw", bufs=10)
-            src = sens[256 * h : 256 * (h + 1), :]
-            eng.dma_start(out=raw["s", h][:], in_=src.rearrange("(n p) k -> p n k", p=NP))
+            src = sens[HALF * h : HALF * (h + 1), :]
+            eng.dma_start(out=raw_tile(("sens", h), [NP, 2, S])[:], in_=src.rearrange("(n p) k -> p n k", p=NP))
 
         def clear(eng, which):
             eng.memset({"mode": mode_rows_t, "query": query_rows, "warm": warm}[which][:], 0.0)
@@ -85,27 +103,18 @@ def tile_gated_deeponet_meet_f5_kernel(
             eng.dma_start(out=mode_rows[row : row + 2, :], in_=vec.rearrange("(g k) -> g k", g=2))
 
         def load_query_rows(eng, row):
-            vec = {0: dist, 16: lift}[row]
-            eng.dma_start(out=query_rows[row : row + 16, :], in_=vec.rearrange("(n p) -> n p", p=NP))
+            vec = {DIST: dist, LIFT: lift}[row]
+            eng.dma_start(out=query_rows[row : row + TILES, :], in_=vec.rearrange("(n p) -> n p", p=NP))
 
         def warm_up(eng):
             eng.activation(out=warm_out[:], in_=warm[:], func=ACT.Sigmoid)
 
-        def identity32(eng):
-            make_identity(nc, ident32[:])
-
-        def identity16(eng):
-            make_identity(nc, ident16[:])
-
-        def copy_on(eng, dst, src):
-            if eng is scalar:
-                eng.copy(out=dst, in_=src)
-            else:
-                eng.tensor_copy(out=dst, in_=src)
+        def identity(eng, dtype):
+            make_identity(nc, {"float32": ident32, "bfloat16": ident16}[dtype][:])
 
         def order_mode_rows(eng):
-            dst = mode_rows_t[0:10, :].rearrange("r (t a i) -> r t a i", t=4, i=4)
-            copy_on(eng, dst, mode_rows[0:10, :].rearrange("r (a t i) -> r t a i", t=4, i=4))
+            dst = mode_rows_t[0:MODE_ROWS, :].rearrange("r (t a i) -> r t a i", t=4, i=4)
+            copy_on(eng, dst, mode_rows[0:MODE_ROWS, :].rearrange("r (a t i) -> r t a i", t=4, i=4))
 
         def turn_mode_rows(eng):
             bank["mode"] = psum_keep.tile([NP, 2 * W], BF16, name="mode_bank")
@@ -114,69 +123,57 @@ def tile_gated_deeponet_meet_f5_kernel(
                 eng.transpose(bank["mode"][:, cols], mode_rows_t[:, cols], ident16[:])
 
         def gather_mode(eng):
-            copy_on(eng, mode_vec[:], bank["mode"][:, 0:W].rearrange("p (t r) -> p r t", t=4)[:, 0:16, :])
+            copy_on(eng, mode_vec[:], bank["mode"][:, 0:W].rearrange("p (t r) -> p r t", t=4)[:, 0:MODE_ROWS, :])
 
         def make_tanh_bias(eng):
-            eng.tensor_tensor(
-                out=tanh_bias[:], in0=mode_vec[:, SLOPE : SLOPE + 2, :], in1=mode_vec[:, C_TRUNK : C_TRUNK + 2, :], op=ALU.mult
-            )
+            in0, in1 = mode_vec[:, SLOPE : SLOPE + 2, :], mode_vec[:, C_TRUNK : C_TRUNK + 2, :]
+            eng.tensor_tensor(out=tanh_bias[:], in0=in0, in1=in1, op=ALU.mult)
 
         def turn_query_rows(eng):
-            bank["query"] = new_bank(BF16)
+            bank["query"] = psum.tile([NP, 2 * W], BF16, name="bank", tag="bank")
             eng.transpose(bank["query"][:, 0:NP], query_rows[:], ident16[:])
 
         def gather_query(eng):
-            eng.activation(out=dist_scaled[:], in_=bank["query"][:, 0:16], func=ACT.Copy, scale=1.0 / 32.0)
-            eng.copy(out=query_vec[:, 16:32], in_=bank["query"][:, 16:32])
+            eng.activation(out=dist_vec[:], in_=bank["query"][:, DIST : DIST + TILES], func=ACT.Copy, scale=INV_SQRT_P)
+            eng.copy(out=lift_vec[:], in_=bank["query"][:, LIFT : LIFT + TILES])
 
-        def interleave(eng, w, s, g, t0, nt):
-            t1 = t0 + nt
-            if (w, s, g) not in grouped:
-                new_grouped((w, s, g))
-            dst = grouped[w, s, g][:].rearrange("p (t a i j) -> p t a j i", t=4, i=4, j=4)
-            src = raw[w, s, g][:].rearrange("p j (a t i) -> p t a j i", t=4, i=4)
+        def lay_weight(eng, name, s, g, t0, nt):
+            dst = rows_tile((name, s, g))[:].rearrange("p (t a i j) -> p t a j i", t=4, i=4, j=4)
+            src = raw[name, s, g][:].rearrange("p j (a t i) -> p t a j i", t=4, i=4)
             if eng is scalar:
-                for t in range(t0, t1):
+                for t in range(t0, t0 + nt):
                     eng.copy(out=dst[:, t], in_=src[:, t])
             else:
-                eng.tensor_copy(out=dst[:, t0:t1], in_=src[:, t0:t1])
+                eng.tensor_copy(out=dst[:, t0 : t0 + nt], in_=src[:, t0 : t0 + nt])
 
         def release(eng, k):
             eng.memset(ones[:, k : k + 1], 1.0)
 
         def release_amp(eng, k, g):
-            eng.tensor_copy(out=amp_late[:, k, :], in_=bank["mode"][:, AMP + g : W : NP])
+            eng.tensor_copy(out=amp_copies[:, k, :], in_=bank["mode"][:, AMP + g : W : NP])
 
-        def pool_interleave(eng, key, t, k):
-            if key not in grouped:
-                new_grouped(key)
+        def lay_quarter(eng, key, t, k):
+            dst = rows_tile(key)[:, W * t : W * (t + 1)]
             if key[0] == "beta":
-                src = grouped["flat", key[1]][:].rearrange("p (t m b) -> p m b t", t=4, m=4)[:, t]
-                dst = grouped[key][:, W * t : W * (t + 1)].rearrange("p (b t) -> p b t", t=4)
+                src = rows["flat", key[1]][:].rearrange("p (t m b) -> p m b t", t=4, m=4)[:, t]
+                dst = dst.rearrange("p (b t) -> p b t", t=4)
             else:
                 src = raw[key][:].rearrange("p j (a t i) -> p t a i j", t=4, i=4)[:, t]
-                dst = grouped[key][:, W * t : W * (t + 1)].rearrange("p (a i j) -> p a i j", i=4, j=4)
+                dst = dst.rearrange("p (a i j) -> p a i j", i=4, j=4)
             eng.tensor_scalar(out=dst, in0=src, scalar1=ones[:, k : k + 1], scalar2=0.0, op0=ALU.mult, op1=ALU.add)
 
-        def pool_tau(eng, c, g, q0, w, k):
-            if ("tau", c, g) not in grouped:
-                new_grouped(("tau", c, g))
-            dst = grouped["tau", c, g][:, 4 * q0 : 4 * (q0 + w)].rearrange("p (q t) -> p q t", t=4)
-            src = act32["th", c, g][:, :, q0 : q0 + w].rearrange("p t q -> p q t")
-            gain = amp_late[:, k, :].unsqueeze(1).broadcast_to([NP, w, 4])
-            eng.tensor_tensor(out=dst, in0=src, in1=gain, op=ALU.mult)
-
-        def quantize(eng, key, q0, w):
+        def quantize(eng, key, lo, w):
             if key not in codes:
-                codes[key] = keep.tile([NP, W], U32, name="codes_" + "_".join(map(str, key)), align_bytes=64)
-                scales[key] = keep.tile([NP, W], U8, name="scales_" + "_".join(map(str, key)), align_bytes=64)
+                label = "_".join(map(str, key))
+                codes[key] = keep.tile([NP, W], U32, name="codes_" + label, align_bytes=64)
+                scales[key] = keep.tile([NP, W], U8, name="scales_" + label, align_bytes=64)
             eng.quantize_mx(
-                out=codes[key][:, q0 : q0 + w].bitcast(FP8X4),
-                scales=scales[key][:, q0 : q0 + w],
-                in_=grouped[key][:, 4 * q0 : 4 * (q0 + w)],
+                out=codes[key][:, lo : lo + w].bitcast(FP8X4),
+                scales=scales[key][:, lo : lo + w],
+                in_=rows[key][:, 4 * lo : 4 * (lo + w)],
             )
 
-        def mx(eng, ps, lhs, m0, rhs, lo, w, start, stop):
+        def mx_pass(eng, ps, lhs, m0, rhs, lo, w, start, stop):
             eng.matmul_mx(
                 out=ps[:, 0:w],
                 lhsT=codes[lhs][:, m0 : m0 + NP].bitcast(FP8X4),
@@ -188,21 +185,19 @@ def tile_gated_deeponet_meet_f5_kernel(
             )
 
         def turn(eng, key, h):
-            if key[0] == "f":
+            if key[0] == "feat":
                 words = raw[key][:, h, :].bitcast(F32).rearrange("p (n k) -> p n k", n=2)
             else:
-                words = raw["s", h][:, :, KP * key[1] : KP * (key[1] + 1)].bitcast(F32)
+                words = raw["sens", h][:, :, W * key[1] : W * (key[1] + 1)].bitcast(F32)
             bank[key, h] = new_bank()
             for n in range(2):
                 for u in range(2):
                     col = NP * (2 * n + u)
-                    eng.transpose(bank[key, h][:, col : col + NP], words[:, n, u:256:2], ident32[:])
+                    eng.transpose(bank[key, h][:, col : col + NP], words[:, n, u:HALF:2], ident32[:])
 
         def gather(eng, key, h):
-            if key not in grouped:
-                new_grouped(key)
-            words = grouped[key][:, 1024 * h : 1024 * (h + 1)].bitcast(F32)
-            if key[0] == "f":
+            words = rows_tile(key)[:, 2 * W * h : 2 * W * (h + 1)].bitcast(F32)
+            if key[0] == "feat":
                 dst = words.rearrange("p (r n u) -> p r n u", n=2, u=2)
                 src = bank[key, h][:].rearrange("p (n u r) -> p r n u", n=2, u=2)
             else:
@@ -212,123 +207,103 @@ def tile_gated_deeponet_meet_f5_kernel(
 
         def trunk_mm(eng, c, g, lo, w, t):
             bank["z", c, g, lo, t] = new_bank()
-            mx(eng, bank["z", c, g, lo, t], ("t", 0, g), NP * t, ("f", c), lo, w, True, True)
+            mx_pass(eng, bank["z", c, g, lo, t], ("trunk", 0, g), NP * t, ("feat", c), lo, w, True, True)
 
         def trunk_tanh(eng, c, g, lo, w, t):
-            if ("th", c, g) not in act32:
-                new_act32(("th", c, g))
             eng.activation(
-                out=act32["th", c, g][:, t, lo : lo + w],
+                out=act_tile(("tanh", c, g))[:, t, lo : lo + w],
                 in_=bank["z", c, g, lo, t][:, 0:w],
                 func=ACT.Tanh,
                 bias=tanh_bias[:, g, t : t + 1],
                 scale=mode_vec[:, SLOPE + g, t : t + 1],
             )
 
-        def branch_mm(eng, w, g, t):
-            bank[w, g, t] = new_bank()
+        def branch_mm(eng, name, g, t):
+            bank[name, g, t] = new_bank()
             for s in range(2):
-                mx(eng, bank[w, g, t], (w, s, g), NP * t, ("s", s), 0, W, s == 0, s == 1)
+                mx_pass(eng, bank[name, g, t], (name, s, g), NP * t, ("sens", s), 0, W, s == 0, s == 1)
 
         def gate(eng, g, t):
-            if ("g", g) not in act32:
-                new_act32(("g", g))
-            eng.activation(
-                out=act32["g", g][:, t, :], in_=bank["g", g, t][:], func=ACT.Sigmoid, bias=mode_vec[:, C_GATE + g, t : t + 1]
-            )
+            bias = mode_vec[:, C_GATE + g, t : t + 1]
+            eng.activation(out=act_tile(("gate", g))[:, t, :], in_=bank["gate", g, t][:], func=ACT.Sigmoid, bias=bias)
 
         def gate_value(eng, g, t):
-            if ("flat", g) not in grouped:
-                new_grouped(("flat", g))
             eng.scalar_tensor_tensor(
-                out=grouped["flat", g][:, W * t : W * (t + 1)],
-                in0=bank["v", g, t][:],
+                out=rows_tile(("flat", g))[:, W * t : W * (t + 1)],
+                in0=bank["val", g, t][:],
                 scalar=mode_vec[:, C_VAL + g, t : t + 1],
-                in1=act32["g", g][:, t, :],
+                in1=act32["gate", g][:, t, :],
                 op0=ALU.add,
                 op1=ALU.mult,
             )
 
-        def by_four(ap, q0, w):
-            return ap[:, :, q0 : q0 + w].rearrange("p t (m i) -> p m t i", i=4)
+        def by_runs(ap, lo, w, run):
+            return ap[:, :, lo : lo + w].rearrange("p t (m i) -> p m t i", i=run)
 
-        def words_by_four(key, q0, w):
-            return grouped[key][:, 4 * q0 : 4 * (q0 + w)].rearrange("p (m i t) -> p m t i", i=4, t=4)
+        def rows_by_runs(key, lo, w, run):
+            return rows_tile(key)[:, 4 * lo : 4 * (lo + w)].rearrange("p (m i t) -> p m t i", i=run, t=4)
 
-        def interleave_beta_part(eng, g, m0, nm):
-            if ("beta", g) not in grouped:
-                new_grouped(("beta", g))
-            flat = grouped["flat", g][:].rearrange("p (t b) -> p t b", t=4)
-            copy_on(eng, words_by_four(("beta", g), NP * m0, NP * nm), by_four(flat, NP * m0, NP * nm))
+        def lay_beta(eng, g, t0, nt):
+            flat = rows["flat", g][:].rearrange("p (t b) -> p t b", t=4)
+            copy_on(eng, rows_by_runs(("beta", g), NP * t0, NP * nt, 4), by_runs(flat, NP * t0, NP * nt, 4))
 
-        def make_tau(eng, c, g, q0, w):
-            if ("tau", c, g) not in grouped:
-                new_grouped(("tau", c, g))
-            gain = bank["mode"][:, AMP + g : W : NP].unsqueeze(1).unsqueeze(3).broadcast_to([NP, w // 4, 4, 4])
-            eng.tensor_tensor(
-                out=words_by_four(("tau", c, g), q0, w), in0=by_four(act32["th", c, g], q0, w), in1=gain, op=ALU.mult
-            )
+        def make_tau(eng, c, g, lo, w):
+            gain = bank["mode"][:, AMP + g : W : NP].unsqueeze(1).unsqueeze(3).broadcast_to([NP, w // 2, 4, 2])
+            in0 = by_runs(act32["tanh", c, g], lo, w, 2)
+            eng.tensor_tensor(out=rows_by_runs(("tau", c, g), lo, w, 2), in0=in0, in1=gain, op=ALU.mult)
+
+        def share_tau(eng, c, g, lo, w, k):
+            dst = rows_tile(("tau", c, g))[:, 4 * lo : 4 * (lo + w)].rearrange("p (q t) -> p q t", t=4)
+            src = act32["tanh", c, g][:, :, lo : lo + w].rearrange("p t q -> p q t")
+            gain = amp_copies[:, k, :].unsqueeze(1).broadcast_to([NP, w, 4])
+            eng.tensor_tensor(out=dst, in0=src, in1=gain, op=ALU.mult)
 
         def field_mm(eng, n, lo, w):
-            bank["o", n, lo] = new_bank()
+            bank["field", n, lo] = new_bank()
             for g in range(2):
-                mx(eng, bank["o", n, lo], ("tau", n // 4, g), NP * (n % 4), ("beta", g), lo, w, g == 0, g == 1)
+                mx_pass(eng, bank["field", n, lo], ("tau", n // 4, g), NP * (n % 4), ("beta", g), lo, w, g == 0, g == 1)
 
         def impose(eng, n, lo, w):
             if n not in turned:
-                turned[n] = work.tile([NP, W], F32, name="turned", tag="turned", bufs=8)
-            dst, src = turned[n][:, lo : lo + w], bank["o", n, lo][:, 0:w]
-            gain, offset = dist_scaled[:, n : n + 1], query_vec[:, 16 + n : 17 + n]
+                turned[n] = work.tile([NP, W], F32, name="turned", tag="turned", bufs=TURNED_BUFS)
+            dst, src = turned[n][:, lo : lo + w], bank["field", n, lo][:, 0:w]
+            gain, offset = dist_vec[:, n : n + 1], lift_vec[:, n : n + 1]
             if eng is scalar:
                 eng.activation(out=dst, in_=src, func=ACT.Identity, bias=offset, scale=gain)
             else:
                 eng.tensor_scalar(out=dst, in0=src, scalar1=gain, scalar2=offset, op0=ALU.mult, op1=ALU.add)
 
         def turn_back(eng, n0, nn, b0, nb):
-            bank["r", n0, b0] = new_bank()
+            bank["out", n0, b0] = new_bank()
             for k in range(nb):
                 for n in range(nn):
                     col = NP * (nn * k + n)
                     src = turned[n0 + n][:, NP * (b0 + k) : NP * (b0 + k + 1)]
-                    eng.transpose(bank["r", n0, b0][:, col : col + NP], src, ident32[:])
+                    eng.transpose(bank["out", n0, b0][:, col : col + NP], src, ident32[:])
 
         def unload(eng, n0, nn, b0, nb):
-            result[n0, b0] = work.tile([NP, W], F32, name="res", tag="res", bufs=9)
-            copy_on(eng, result[n0, b0][:, 0 : NP * nn * nb], bank["r", n0, b0][:, 0 : NP * nn * nb])
+            result[n0, b0] = work.tile([NP, W], F32, name="result", tag="result", bufs=RESULT_BUFS)
+            copy_on(eng, result[n0, b0][:, 0 : NP * nn * nb], bank["out", n0, b0][:, 0 : NP * nn * nb])
 
         def store(eng, n0, nn, b0, nb):
             dst = out[NP * b0 : NP * (b0 + nb), NP * n0 : NP * (n0 + nn)].rearrange("(k p) q -> p k q", p=NP)
             eng.dma_start(out=dst, in_=result[n0, b0][:, 0 : NP * nn * nb].rearrange("p (k q) -> p k q", k=nb))
 
-        result = {}
 
-        def four(fn, *a):
-            return [(fn, *a, t) for t in range(4)]
+        def four(fn, *args):
+            return [(fn, *args, t) for t in range(4)]
 
-        def halves(fn, key):
+        def halves(fn, *key):
             return [(fn, key, h) for h in range(2)]
 
-        def lay(w, s, g):
-            return (interleave, w, s, g, 0, 4)
+        def lay(name, s, g, t0=0, nt=4):
+            return (lay_weight, name, s, g, t0, nt)
 
-        def quant(*key):
-            return (quantize, key, 0, W)
+        def quant(*key, lo=0, w=W):
+            return (quantize, key, lo, w)
 
-        def tau(c, g, q0=0, w=W):
-            return (make_tau, c, g, q0, w)
-
-        def qtau(c, g, q0=0, w=W):
-            return (quantize, ("tau", c, g), q0, w)
-
-
-        def banks_of(fn, n0, nn):
-            return [(fn, n0, nn, b0, 4 // nn) for b0 in range(0, 4, 4 // nn)]
-
-        def imposes(n0, n1):
-            return [(impose, n, 0, W) for n in range(n0, n1)]
-
-        def fields(n0, n1):
-            return [(field_mm, n, 0, W) for n in range(n0, n1)]
+        def tau(c, g, lo=0, w=W):
+            return (make_tau, c, g, lo, w)
 
         def tanhs(c, g, lo=0, w=W):
             return four(trunk_tanh, c, g, lo, w)
@@ -336,140 +311,174 @@ def tile_gated_deeponet_meet_f5_kernel(
         def zs(c, g, lo=0, w=W):
             return four(trunk_mm, c, g, lo, w)
 
-        def pooled(key, k, ts=range(4)):
-            return [(pool_interleave, key, t, k) for t in ts]
+        def tiles(fn, n0, n1):
+            return [(fn, n, 0, W) for n in range(n0, n1)]
 
-        def part(w, s, g, t0, nt):
-            return (interleave, w, s, g, t0, nt)
+        def quarters(key, ts, k):
+            return [(lay_quarter, key, t, k) for t in ts]
 
-        def qpart(key, lo, w):
-            return (quantize, key, lo, w)
+        chunk_blocks = [[(4 * c, 4, b, 1) for b in range(4)] for c in range(3)]
+        pair_blocks = [(12, 2, b, 2) for b in (0, 2)]
+        last_blocks = [(14, 2, b, 1) for b in range(4)]
 
-        sync_order = [(load_feat, 0, 0, 1)] + [(load_mode_rows, row) for row in (C_TRUNK, SLOPE, AMP, C_VAL, C_GATE)]
-        sync_order += [(load_weight, "t", 0, 0), (load_feat, 0, 1, 1), (load_weight, "t", 0, 1), (load_query_rows, 0), (load_query_rows, 16)]
-        sync_order += [(load_weight, "g", 0, 0), (load_weight, "g", 1, 0), (load_sens, 0), (load_feat, 1, 0, 2), (load_weight, "v", 0, 0), (load_sens, 1)]
-        sync_order += [(load_weight, "v", 1, 0), (load_weight, "g", 0, 1), (load_feat, 2, 0, 2), (load_weight, "g", 1, 1), (load_weight, "v", 1, 1)]
-        sync_order += [(load_weight, "v", 0, 1), (load_feat, 3, 0, 2)]
-        sync_order += banks_of(store, 0, 4) + banks_of(store, 4, 4) + banks_of(store, 8, 4) + banks_of(store, 12, 2) + [(store, 14, 2, b0, 1) for b0 in range(4)]
-
-        pool_order = [(clear, "warm"), (identity32,), (identity16,)]
-        pool_order += pooled(("g", 1, 0), 0) + pooled(("v", 0, 0), 0, [0]) + pooled(("g", 1, 1), 1, [0, 1]) + pooled(("v", 1, 1), 2) + pooled(("beta", 0), 3, [0, 1])
-        pool_order += [(pool_tau, 1, 1, 0, 256, 0), (pool_tau, 2, 1, 0, 256, 1), (pool_tau, 3, 1, 0, 256, 2)]
-
-        scalar_order = [(warm_up,), (order_mode_rows,), part("t", 0, 0, 0, 2), (gather_mode,), (gather, ("f", 0), 1), part("t", 0, 1, 0, 2)]
-        scalar_order += tanhs(0, 0, 0, 256) + tanhs(0, 0, 256, 256) + tanhs(0, 1) + halves(gather, ("f", 1)) + [part("v", 0, 0, 1, 3)]
-        scalar_order += [(gather, ("s", 0), 1)] + halves(gather, ("s", 1)) + tanhs(1, 0) + halves(gather, ("f", 2)) + [(gather_query,)] + tanhs(1, 1)
-        scalar_order += [part("g", 1, 1, 2, 2)] + four(gate, 0) + [lay("v", 0, 1)] + tanhs(2, 0)[:2] + [(gather, ("f", 3), 1)] + four(gate, 1)
-        scalar_order += [(interleave_beta_part, 0, 2, 2)] + tanhs(2, 0)[2:] + tanhs(2, 1) + tanhs(3, 1)[:2] + imposes(0, 2) + tanhs(3, 1)[2:] + tanhs(3, 0)
-        scalar_order += imposes(7, 8) + banks_of(unload, 0, 4) + imposes(8, 11) + banks_of(unload, 4, 4)[:3] + banks_of(unload, 8, 4)[:1]
-        scalar_order += imposes(12, 15) + [(unload, 8, 4, 3, 1), (unload, 12, 2, 2, 2), (unload, 14, 2, 0, 1), (unload, 14, 2, 2, 1)]
-
-        vector_order = [(clear, "mode"), (clear, "query"), (gather, ("f", 0), 0), qpart(("f", 0), 0, 256), part("t", 0, 0, 2, 2), qpart(("t", 0, 0), 0, 256), (make_tanh_bias,)]
-        vector_order += [qpart(("t", 0, 0), 256, 256), part("t", 0, 1, 2, 2), qpart(("f", 0), 256, 256), lay("g", 0, 0), quant("t", 0, 1), quant("g", 0, 0)]
-        vector_order += [(release, 0), tau(0, 0), (gather, ("s", 0), 0), tau(0, 1), quant("f", 1), lay("v", 1, 0), quant("s", 0), quant("g", 1, 0), quant("s", 1)]
-        vector_order += [lay("g", 0, 1), quant("v", 1, 0), quant("v", 0, 0), quant("g", 0, 1), (release, 1), tau(1, 0), qtau(0, 0), quant("g", 1, 1), quant("f", 2)]
-        vector_order += [(release, 2)] + four(gate_value, 0) + [tau(1, 1, 256, 256), (gather, ("f", 3), 0), quant("v", 0, 1), quant("v", 1, 1), quant("f", 3), qtau(1, 0)]
-        vector_order += [(release, 3)] + four(gate_value, 1) + [qtau(0, 1), (interleave_beta_part, 1, 0, 4), quant("beta", 0), quant("beta", 1)]
-        vector_order += [(release_amp, 0, 1), tau(2, 0)] + imposes(2, 3) + [qtau(2, 0), qtau(1, 1)]
-        vector_order += [(release_amp, 1, 1), tau(2, 1, 256, 256)] + imposes(3, 7) + [qtau(2, 1)]
-        vector_order += [(release_amp, 2, 1), tau(3, 1, 256, 256), tau(3, 0)] + imposes(11, 12) + [qtau(3, 0), qtau(3, 1)]
-        vector_order += [(unload, 4, 4, 3, 1), (unload, 8, 4, 1, 1), (unload, 8, 4, 2, 1)] + imposes(15, 16) + [(unload, 12, 2, 0, 2), (unload, 14, 2, 1, 1), (unload, 14, 2, 3, 1)]
-
-        tensor_order = [(turn, ("f", 0), 0), (turn_mode_rows,), (turn, ("f", 0), 1)] + zs(0, 0, 0, 256) + [(turn_query_rows,)] + zs(0, 0, 256, 256)
-        tensor_order += zs(0, 1) + [(turn, ("s", 0), 0)] + halves(turn, ("f", 1)) + [(turn, ("s", 0), 1)] + halves(turn, ("s", 1)) + zs(1, 0)
-        tensor_order += halves(turn, ("f", 2)) + zs(1, 1) + four(branch_mm, "g", 0) + four(branch_mm, "v", 0) + four(branch_mm, "g", 1)[:2]
-        tensor_order += halves(turn, ("f", 3)) + zs(2, 0)[:2] + four(branch_mm, "g", 1)[2:] + four(branch_mm, "v", 1) + zs(2, 0)[2:] + zs(2, 1) + zs(3, 1)[:2]
-        tensor_order += fields(0, 4) + zs(3, 1)[2:] + zs(3, 0) + fields(4, 8) + banks_of(turn_back, 0, 4) + fields(8, 12)
-        tensor_order += banks_of(turn_back, 4, 4) + banks_of(turn_back, 8, 4)[:3] + fields(12, 16) + banks_of(turn_back, 8, 4)[3:]
-        tensor_order += banks_of(turn_back, 12, 2) + [(turn_back, 14, 2, b0, 1) for b0 in range(4)]
-
-        programs = [(gpsimd, pool_order), (sync, sync_order), (vector, vector_order), (scalar, scalar_order), (tensor, tensor_order)]
+        def blocks(fn, which):
+            return [(fn, *block) for block in which]
 
 
-        steps = [st for (eng, order) in programs for st in order]
+        sync_order = [(load_feat, 0, 0, 1), (load_feat, 0, 1, 1)]
+        sync_order += [(load_mode_rows, row) for row in (C_TRUNK, SLOPE, AMP, C_VAL, C_GATE)]
+        sync_order += [(load_weight, "trunk", 0, 0), (load_weight, "trunk", 0, 1), (load_weight, "gate", 0, 0)]
+        sync_order += [(load_weight, "gate", 1, 0), (load_feat, 1, 0, 2), (load_weight, "val", 0, 0)]
+        sync_order += [(load_query_rows, DIST), (load_weight, "gate", 0, 1), (load_sens, 0), (load_sens, 1)]
+        sync_order += [(load_feat, 2, 0, 2), (load_weight, "val", 1, 0), (load_feat, 3, 0, 2), (load_query_rows, LIFT)]
+        sync_order += [(load_weight, "gate", 1, 1), (load_weight, "val", 1, 1), (load_weight, "val", 0, 1)]
+        for which in chunk_blocks + [pair_blocks, last_blocks]:
+            sync_order += blocks(store, which)
+
+        vector_order = [(clear, "mode"), (order_mode_rows,), (clear, "query"), lay("trunk", 0, 0, 2, 2), (make_tanh_bias,)]
+        vector_order += [quant("feat", 0, w=HALF), quant("trunk", 0, 0, lo=HALF, w=HALF), quant("feat", 0, lo=HALF, w=HALF)]
+        vector_order += [lay("trunk", 0, 1, 0, 2), quant("trunk", 0, 0, w=HALF), lay("gate", 0, 0), quant("trunk", 0, 1)]
+        vector_order += [(release, 0), quant("gate", 0, 0), tau(0, 0)] + halves(gather, "feat", 1) + [tau(0, 1)]
+        vector_order += [quant("feat", 1), quant("tau", 0, 1), quant("gate", 1, 0), quant("sens", 0), quant("val", 0, 0)]
+        vector_order += [quant("sens", 1), lay("val", 1, 0)]
+        vector_order += [(release, 1), quant("gate", 0, 1), tau(1, 0), quant("val", 1, 0), quant("gate", 1, 1)]
+        vector_order += [(release, 2), quant("feat", 2)]
+        for h in range(2):
+            vector_order += [(gather, ("feat", 3), h)] + four(gate_value, 0)[2 * h : 2 * h + 2]
+        vector_order += [tau(1, 1, HALF, HALF), quant("val", 0, 1), quant("val", 1, 1), quant("feat", 3)]
+        vector_order += [(release, 3), quant("tau", 1, 0)] + four(gate_value, 1)
+        vector_order += [quant("tau", 0, 0), (lay_beta, 1, 0, 4), quant("beta", 0)]
+        vector_order += [(release_amp, 0, 1), quant("beta", 1), tau(2, 0)] + tiles(impose, 0, 1) + [quant("tau", 1, 1)]
+        vector_order += [(release_amp, 1, 1), quant("tau", 2, 0), tau(2, 1, HALF, HALF)] + tiles(impose, 4, 7)
+        vector_order += [(release_amp, 2, 1), quant("tau", 2, 1), tau(3, 0), quant("tau", 3, 0)]
+        vector_order += [(release_amp, 3, 1), quant("tau", 3, 1, w=HALF)] + tiles(impose, 10, 13)
+        vector_order += blocks(unload, chunk_blocks[2][:2])
+        vector_order += [quant("tau", 3, 1, lo=2 * NP, w=NP), quant("tau", 3, 1, lo=3 * NP, w=NP)]
+        vector_order += blocks(unload, pair_blocks[:1]) + tiles(impose, 14, 15)
+        vector_order += [(impose, 15, 0, HALF), (impose, 15, HALF, HALF)] + blocks(unload, last_blocks[1::2])
+
+        gpsimd_order = [(clear, "warm"), (identity, "float32"), (identity, "bfloat16")]
+        gpsimd_order += quarters(("gate", 1, 0), range(4), 0) + quarters(("val", 0, 0), range(2), 0)
+        gpsimd_order += quarters(("gate", 1, 1), range(2), 1)
+        gpsimd_order += quarters(("val", 0, 1), range(1), 2) + quarters(("val", 1, 1), range(4), 2)
+        gpsimd_order += quarters(("beta", 0), range(3), 3)
+        gpsimd_order += [(share_tau, c, 1, 0, HALF, c - 1) for c in (1, 2, 3)]
+        gpsimd_order += [(share_tau, 3, 1, NP * n, NP, 3) for n in (2, 3)]
+
+        scalar_order = [(warm_up,)] + halves(gather, "feat", 0) + [(gather_mode,)]
+        scalar_order += [lay("trunk", 0, 0, 0, 2), lay("trunk", 0, 1, 2, 2)]
+        for ts in (slice(2, 4), slice(0, 2)):
+            scalar_order += tanhs(0, 0, 0, HALF)[ts] + tanhs(0, 0, HALF, HALF)[ts]
+        scalar_order += tanhs(0, 1) + [lay("val", 0, 0, 2, 2), lay("gate", 0, 1)]
+        scalar_order += halves(gather, "sens", 0) + halves(gather, "sens", 1) + tanhs(1, 0)
+        scalar_order += [(gather, ("feat", 2), 0), lay("gate", 1, 1, 2, 2), (gather, ("feat", 2), 1)]
+        scalar_order += four(gate, 0)[:2] + tanhs(1, 1)[:2] + four(gate, 0)[2:] + tanhs(1, 1)[2:]
+        scalar_order += [lay("val", 0, 1, 1, 3)] + four(gate, 1) + [(gather_query,)] + tanhs(2, 0) + [(lay_beta, 0, 3, 1)]
+        scalar_order += tanhs(3, 1)[:2] + tanhs(2, 1)[:2] + tanhs(3, 1)[2:] + tanhs(3, 0)[:2] + tanhs(2, 1)[2:]
+        scalar_order += tiles(impose, 1, 4) + tanhs(3, 0)[2:] + tiles(impose, 7, 8)
+        scalar_order += blocks(unload, chunk_blocks[0] + chunk_blocks[1][:1]) + tiles(impose, 8, 10)
+        scalar_order += blocks(unload, chunk_blocks[1][1:]) + tiles(impose, 13, 14)
+        scalar_order += blocks(unload, chunk_blocks[2][2:] + pair_blocks[1:] + last_blocks[0::2])
+
+        tensor_order = halves(turn, "feat", 0) + [(turn_mode_rows,)]
+        for ts in (slice(2, 4), slice(0, 2)):
+            tensor_order += zs(0, 0, 0, HALF)[ts] + zs(0, 0, HALF, HALF)[ts]
+        tensor_order += zs(0, 1) + halves(turn, "feat", 1) + halves(turn, "sens", 0) + halves(turn, "sens", 1)
+        tensor_order += zs(1, 0) + halves(turn, "feat", 2) + halves(turn, "feat", 3)
+        tensor_order += four(branch_mm, "gate", 0)[:2] + zs(1, 1)[:2] + four(branch_mm, "gate", 0)[2:]
+        tensor_order += four(branch_mm, "val", 0)[:2] + zs(1, 1)[2:] + four(branch_mm, "val", 0)[2:]
+        tensor_order += zs(2, 0)[:2] + [(turn_query_rows,)] + four(branch_mm, "gate", 1) + zs(2, 0)[2:]
+        tensor_order += four(branch_mm, "val", 1) + zs(3, 1)[:2] + zs(3, 0)[:2] + zs(3, 1)[2:] + zs(2, 1)
+        tensor_order += tiles(field_mm, 0, 4) + zs(3, 0)[2:] + tiles(field_mm, 4, 8)
+        tensor_order += blocks(turn_back, chunk_blocks[0] + chunk_blocks[1]) + tiles(field_mm, 8, 14)
+        tensor_order += blocks(turn_back, chunk_blocks[2] + pair_blocks[:1]) + tiles(field_mm, 14, 15)
+        tensor_order += [(field_mm, 15, 0, HALF)] + blocks(turn_back, pair_blocks[1:]) + [(field_mm, 15, HALF, HALF)]
+        tensor_order += blocks(turn_back, last_blocks)
+
+
+        programs = [
+            (gpsimd, gpsimd_order),
+            (sync, sync_order),
+            (vector, vector_order),
+            (scalar, scalar_order),
+            (tensor, tensor_order),
+        ]
+        steps = [step for eng, order in programs for step in order]
+
 
         def covering(fn, key, lo, hi):
             n = len(key) + 1
             return [st for st in steps if st[0] is fn and st[1:n] == key and st[n] < hi and st[n] + st[n + 1] > lo]
 
-        def inputs(step):
-            fn, a = step[0], step[1:]
-            if fn is load_query_rows:
-                return [(clear, "query")]
-            if fn is warm_up:
-                return [(clear, "warm")]
-            if fn is order_mode_rows:
-                return [(clear, "mode")] + [st for st in steps if st[0] is load_mode_rows]
-            if fn is turn_mode_rows:
-                return [(order_mode_rows,), (identity16,)]
-            if fn is gather_mode:
-                return [(turn_mode_rows,)]
-            if fn is make_tanh_bias:
-                return [(gather_mode,)]
-            if fn is turn_query_rows:
-                return [(load_query_rows, 0), (load_query_rows, 16), (identity16,)]
-            if fn is gather_query:
-                return [(turn_query_rows,)]
-            if fn is interleave:
-                return [(load_weight, *a[:3])]
-            if fn is release_amp:
-                return [(gather_mode,)]
-            if fn is pool_interleave:
-                return [(release, a[2])] + ([(gate_value, a[0][1], t) for t in range(4)] if a[0][0] == "beta" else [(load_weight, *a[0])])
-            if fn is pool_tau:
-                return [(release_amp, a[4], a[1])] + covering(trunk_tanh, a[:2], a[2], a[2] + a[3])
-            if fn is turn:
-                loads = covering(load_feat, a[0][1:], a[1], a[1] + 1) if a[0][0] == "f" else [(load_sens, a[1])]
-                return [(identity32,)] + loads
-            if fn is gather:
-                return [(turn, *a)]
-            if fn is quantize:
-                key, lo, hi = a[0], a[1], a[1] + a[2]
-                if key[0] in ("f", "s"):
-                    return [(gather, key, h) for h in range(lo // 256, hi // 256)]
-                pooled = [st for st in steps if st[0] is pool_interleave and st[1] == key and lo <= NP * st[2] < hi]
-                if key[0] == "beta":
-                    return pooled + covering(interleave_beta_part, key[1:], 0, 4)
-                if key[0] == "tau":
-                    return covering(make_tau, key[1:], lo, hi) + covering(pool_tau, key[1:], lo, hi)
-                return pooled + covering(interleave, key, lo // NP, hi // NP)
-            if fn is trunk_mm:
-                c, g, lo, w, t = a
-                return covering(quantize, (("t", 0, g),), NP * t, NP * t + NP) + covering(quantize, (("f", c),), lo, lo + w)
-            if fn is trunk_tanh:
-                return [(trunk_mm, *a), (make_tanh_bias,)]
-            if fn is branch_mm:
-                return [st for s in range(2) for key in ((a[0], s, a[1]), ("s", s)) for st in covering(quantize, (key,), 0, W)]
-            if fn is gate:
-                return [(branch_mm, "g", *a), (gather_mode,)]
-            if fn is gate_value:
-                return [(branch_mm, "v", *a), (gate, *a)]
-            if fn is interleave_beta_part:
-                return [(gate_value, a[0], t) for t in range(4)]
-            if fn is make_tau:
-                return [(gather_mode,)] + covering(trunk_tanh, a[:2], a[2], a[2] + a[3])
-            if fn is field_mm:
-                lo = NP * (a[0] % 4)
-                taus = [st for g in range(2) for st in covering(quantize, (("tau", a[0] // 4, g),), lo, lo + NP)]
-                return taus + [(quantize, ("beta", g), 0, W) for g in range(2)]
-            if fn is impose:
-                return [(field_mm, *a), (gather_query,)]
-            if fn is turn_back:
-                n0, nn, b0, nb = a
-                return [st for n in range(n0, n0 + nn) for st in covering(impose, (n,), NP * b0, NP * (b0 + nb))]
-            if fn is unload:
-                return [(turn_back, *a)]
-            if fn is store:
-                return [(unload, *a)]
-            return []
+        def quantized(key, lo=0, hi=W):
+            return covering(quantize, (key,), lo, hi)
+
+        def writers_of_rows(key, lo, w):
+            kind = key[0]
+            if kind in ("feat", "sens"):
+                return [(gather, key, h) for h in range(lo // HALF, (lo + w) // HALF)]
+            if kind == "tau":
+                return covering(make_tau, key[1:], lo, lo + w) + covering(share_tau, key[1:], lo, lo + w)
+            shared = [st for st in steps if st[0] is lay_quarter and st[1] == key and lo <= NP * st[2] < lo + w]
+            if kind == "beta":
+                return shared + covering(lay_beta, key[1:], lo // NP, (lo + w) // NP)
+            return shared + covering(lay_weight, key, lo // NP, (lo + w) // NP)
+
+        def unlaid(key):
+            return four(gate_value, key[1]) if key[0] == "beta" else [(load_weight, *key)]
+
+        def unturned(key, h):
+            return covering(load_feat, key[1:], h, h + 1) if key[0] == "feat" else [(load_sens, h)]
+
+        inputs = {
+            load_query_rows: lambda row: [(clear, "query")],
+            warm_up: lambda: [(clear, "warm")],
+            order_mode_rows: lambda: [(clear, "mode")] + [st for st in steps if st[0] is load_mode_rows],
+            turn_mode_rows: lambda: [(order_mode_rows,), (identity, "bfloat16")],
+            gather_mode: lambda: [(turn_mode_rows,)],
+            make_tanh_bias: lambda: [(gather_mode,)],
+            turn_query_rows: lambda: [(load_query_rows, DIST), (load_query_rows, LIFT), (identity, "bfloat16")],
+            gather_query: lambda: [(turn_query_rows,)],
+            lay_weight: lambda name, s, g, t0, nt: [(load_weight, name, s, g)],
+            release_amp: lambda k, g: [(gather_mode,)],
+            lay_quarter: lambda key, t, k: [(release, k)] + unlaid(key),
+            quantize: writers_of_rows,
+            turn: lambda key, h: [(identity, "float32")] + unturned(key, h),
+            gather: lambda key, h: [(turn, key, h)],
+            trunk_mm: lambda c, g, lo, w, t: quantized(("trunk", 0, g), NP * t, NP * (t + 1))
+            + quantized(("feat", c), lo, lo + w),
+            trunk_tanh: lambda *args: [(trunk_mm, *args), (make_tanh_bias,)],
+            branch_mm: lambda name, g, t: [
+                st for s in range(2) for key in ((name, s, g), ("sens", s)) for st in quantized(key)
+            ],
+            gate: lambda g, t: [(branch_mm, "gate", g, t), (gather_mode,)],
+            gate_value: lambda g, t: [(branch_mm, "val", g, t), (gate, g, t)],
+            lay_beta: lambda g, t0, nt: four(gate_value, g),
+            make_tau: lambda c, g, lo, w: [(gather_mode,)] + covering(trunk_tanh, (c, g), lo, lo + w),
+            share_tau: lambda c, g, lo, w, k: [(release_amp, k, g)] + covering(trunk_tanh, (c, g), lo, lo + w),
+            field_mm: lambda n, lo, w: [
+                st
+                for g in range(2)
+                for st in quantized(("beta", g)) + quantized(("tau", n // 4, g), NP * (n % 4), NP * (n % 4 + 1))
+            ],
+            impose: lambda *args: [(field_mm, *args), (gather_query,)],
+            turn_back: lambda n0, nn, b0, nb: [
+                st for n in range(n0, n0 + nn) for st in covering(impose, (n,), NP * b0, NP * (b0 + nb))
+            ],
+            unload: lambda *args: [(turn_back, *args)],
+            store: lambda *args: [(unload, *args)],
+        }
+
+        def ready(step):
+            return step[0] not in inputs or all(st in traced for st in inputs[step[0]](*step[1:]))
 
         traced, place = set(), [0] * len(programs)
         while len(traced) < len(steps):
             before = len(traced)
             for e, (eng, order) in enumerate(programs):
-                if place[e] < len(order) and all(st in traced for st in inputs(order[place[e]])):
+                if place[e] < len(order) and ready(order[place[e]]):
                     step = order[place[e]]
                     step[0](eng, *step[1:])
                     traced.add(step)
                     place[e] += 1
-            assert len(traced) > before
+            assert len(traced) > before, "the orders wait for each other"

from contextlib import ExitStack

import concourse.mybir as mybir
from concourse.masks import make_identity

B, S, Q, C, P = 512, 1024, 2048, 512, 1024
FLOPS = 2 * (2 * B * S * P + Q * C * P + B * P * Q)

F32 = mybir.dt.float32
BF16 = mybir.dt.bfloat16
U32 = mybir.dt.uint32
U8 = mybir.dt.uint8
FP8X4 = mybir.dt.float8_e4m3fn_x4
ACT = mybir.ActivationFunctionType
ALU = mybir.AluOpType

NP = 128
W = 512
HALF = W // 2
INV_SQRT_P = 1.0 / 32.0

C_TRUNK, SLOPE, AMP, C_VAL, C_GATE = 0, 2, 4, 6, 8
MODE_ROWS = 10
TILES = Q // NP
DIST, LIFT = 0, TILES

RAW_BUFS, ROWS_BUFS, ACT_BUFS, TURNED_BUFS, RESULT_BUFS, PSUM_BANKS = 10, 7, 8, 8, 9, 7


def tile_gated_deeponet_meet_f5_kernel(
    tc, sens, w_val, c_val, w_gate, c_gate, feat, w_trunk, c_trunk, slope, amp, dist, lift, out
):
    nc = tc.nc
    sync, scalar, vector, gpsimd, tensor = nc.sync, nc.scalar, nc.vector, nc.gpsimd, nc.tensor
    with ExitStack() as ctx:
        keep = ctx.enter_context(tc.tile_pool(name="keep", bufs=1))
        work = ctx.enter_context(tc.tile_pool(name="work", bufs=1))
        psum = ctx.enter_context(tc.psum_pool(name="psum", bufs=PSUM_BANKS))
        psum_keep = ctx.enter_context(tc.psum_pool(name="psum_keep", bufs=1))
        ctx.enter_context(tc.manual_schedule())

        weights = {"trunk": w_trunk, "val": w_val, "gate": w_gate}
        raw, rows, codes, scales = {}, {}, {}, {}
        act32, bank, turned, result = {}, {}, {}, {}

        ident32 = keep.tile([NP, NP], F32, name="ident32")
        ident16 = keep.tile([NP, NP], BF16, name="ident16")
        mode_rows = keep.tile([NP, W], BF16, name="mode_rows")
        mode_rows_t = keep.tile([NP, W], BF16, name="mode_rows_t")
        query_rows = keep.tile([NP, NP], BF16, name="query_rows")
        mode_vec = keep.tile([NP, MODE_ROWS, 4], F32, name="mode_vec")
        tanh_bias = keep.tile([NP, 2, 4], F32, name="tanh_bias")
        lift_vec = keep.tile([NP, TILES], F32, name="lift_vec")
        dist_vec = keep.tile([NP, TILES], F32, name="dist_vec")
        ones = keep.tile([NP, 4], F32, name="ones")
        amp_copies = keep.tile([NP, 4, 4], F32, name="amp_copies")
        warm = keep.tile([NP, 8], F32, name="warm")
        warm_out = keep.tile([NP, 8], F32, name="warm_out")

        def new_bank():
            return psum.tile([NP, W], F32, name="bank", tag="bank")

        def raw_tile(key, shape):
            if key not in raw:
                raw[key] = work.tile(shape, BF16, name="raw", tag="raw", bufs=RAW_BUFS)
            return raw[key]

        def rows_tile(key):
            if key not in rows:
                rows[key] = work.tile([NP, 4 * W], BF16, name="rows", tag="rows", bufs=ROWS_BUFS, align_bytes=64)
            return rows[key]

        def act_tile(key):
            if key not in act32:
                act32[key] = work.tile([NP, 4, W], F32, name="act32", tag="act32", bufs=ACT_BUFS)
            return act32[key]

        def copy_on(eng, dst, src):
            if eng is scalar:
                eng.copy(out=dst, in_=src)
            else:
                eng.tensor_copy(out=dst, in_=src)


        def load_weight(eng, name, s, g):
            src = weights[name][W * s : W * (s + 1), W * g : W * (g + 1)]
            eng.dma_start(out=raw_tile((name, s, g), [NP, 4, W])[:], in_=src.rearrange("(p j) c -> p j c", j=4))

        def load_feat(eng, c, h0, nh):
            src = feat[W * c + HALF * h0 : W * c + HALF * (h0 + nh), :]
            dst = raw_tile(("feat", c), [NP, 2, 2 * C])[:, h0 : h0 + nh, :]
            eng.dma_start(out=dst, in_=src.rearrange("(h p n) k -> p h (n k)", h=nh, n=2))

        def load_sens(eng, h):
            src = sens[HALF * h : HALF * (h + 1), :]
            eng.dma_start(out=raw_tile(("sens", h), [NP, 2, S])[:], in_=src.rearrange("(n p) k -> p n k", p=NP))

        def clear(eng, which):
            eng.memset({"mode": mode_rows_t, "query": query_rows, "warm": warm}[which][:], 0.0)

        def load_mode_rows(eng, row):
            vec = {C_TRUNK: c_trunk, SLOPE: slope, AMP: amp, C_VAL: c_val, C_GATE: c_gate}[row]
            eng.dma_start(out=mode_rows[row : row + 2, :], in_=vec.rearrange("(g k) -> g k", g=2))

        def load_query_rows(eng, row):
            vec = {DIST: dist, LIFT: lift}[row]
            eng.dma_start(out=query_rows[row : row + TILES, :], in_=vec.rearrange("(n p) -> n p", p=NP))

        def warm_up(eng):
            eng.activation(out=warm_out[:], in_=warm[:], func=ACT.Sigmoid)

        def identity(eng, dtype):
            make_identity(nc, {"float32": ident32, "bfloat16": ident16}[dtype][:])

        def order_mode_rows(eng):
            dst = mode_rows_t[0:MODE_ROWS, :].rearrange("r (t a i) -> r t a i", t=4, i=4)
            copy_on(eng, dst, mode_rows[0:MODE_ROWS, :].rearrange("r (a t i) -> r t a i", t=4, i=4))

        def turn_mode_rows(eng):
            bank["mode"] = psum_keep.tile([NP, 2 * W], BF16, name="mode_bank")
            for t in range(4):
                cols = slice(NP * t, NP * (t + 1))
                eng.transpose(bank["mode"][:, cols], mode_rows_t[:, cols], ident16[:])

        def gather_mode(eng):
            copy_on(eng, mode_vec[:], bank["mode"][:, 0:W].rearrange("p (t r) -> p r t", t=4)[:, 0:MODE_ROWS, :])

        def make_tanh_bias(eng):
            in0, in1 = mode_vec[:, SLOPE : SLOPE + 2, :], mode_vec[:, C_TRUNK : C_TRUNK + 2, :]
            eng.tensor_tensor(out=tanh_bias[:], in0=in0, in1=in1, op=ALU.mult)

        def turn_query_rows(eng):
            bank["query"] = psum.tile([NP, 2 * W], BF16, name="bank", tag="bank")
            eng.transpose(bank["query"][:, 0:NP], query_rows[:], ident16[:])

        def gather_query(eng):
            eng.activation(out=dist_vec[:], in_=bank["query"][:, DIST : DIST + TILES], func=ACT.Copy, scale=INV_SQRT_P)
            eng.copy(out=lift_vec[:], in_=bank["query"][:, LIFT : LIFT + TILES])

        def lay_weight(eng, name, s, g, t0, nt):
            dst = rows_tile((name, s, g))[:].rearrange("p (t a i j) -> p t a j i", t=4, i=4, j=4)
            src = raw[name, s, g][:].rearrange("p j (a t i) -> p t a j i", t=4, i=4)
            if eng is scalar:
                for t in range(t0, t0 + nt):
                    eng.copy(out=dst[:, t], in_=src[:, t])
            else:
                eng.tensor_copy(out=dst[:, t0 : t0 + nt], in_=src[:, t0 : t0 + nt])

        def release(eng, k):
            eng.memset(ones[:, k : k + 1], 1.0)

        def release_amp(eng, k, g):
            eng.tensor_copy(out=amp_copies[:, k, :], in_=bank["mode"][:, AMP + g : W : NP])

        def lay_quarter(eng, key, t, k):
            dst = rows_tile(key)[:, W * t : W * (t + 1)]
            if key[0] == "beta":
                src = rows["flat", key[1]][:].rearrange("p (t m b) -> p m b t", t=4, m=4)[:, t]
                dst = dst.rearrange("p (b t) -> p b t", t=4)
            else:
                src = raw[key][:].rearrange("p j (a t i) -> p t a i j", t=4, i=4)[:, t]
                dst = dst.rearrange("p (a i j) -> p a i j", i=4, j=4)
            eng.tensor_scalar(out=dst, in0=src, scalar1=ones[:, k : k + 1], scalar2=0.0, op0=ALU.mult, op1=ALU.add)

        def quantize(eng, key, lo, w):
            if key not in codes:
                label = "_".join(map(str, key))
                codes[key] = keep.tile([NP, W], U32, name="codes_" + label, align_bytes=64)
                scales[key] = keep.tile([NP, W], U8, name="scales_" + label, align_bytes=64)
            eng.quantize_mx(
                out=codes[key][:, lo : lo + w].bitcast(FP8X4),
                scales=scales[key][:, lo : lo + w],
                in_=rows[key][:, 4 * lo : 4 * (lo + w)],
            )

        def mx_pass(eng, ps, lhs, m0, rhs, lo, w, start, stop):
            eng.matmul_mx(
                out=ps[:, 0:w],
                lhsT=codes[lhs][:, m0 : m0 + NP].bitcast(FP8X4),
                lhsT_scale=scales[lhs][:, m0 : m0 + NP],
                rhs=codes[rhs][:, lo : lo + w].bitcast(FP8X4),
                rhs_scale=scales[rhs][:, lo : lo + w],
                start=start,
                stop=stop,
            )

        def turn(eng, key, h):
            if key[0] == "feat":
                words = raw[key][:, h, :].bitcast(F32).rearrange("p (n k) -> p n k", n=2)
            else:
                words = raw["sens", h][:, :, W * key[1] : W * (key[1] + 1)].bitcast(F32)
            bank[key, h] = new_bank()
            for n in range(2):
                for u in range(2):
                    col = NP * (2 * n + u)
                    eng.transpose(bank[key, h][:, col : col + NP], words[:, n, u:HALF:2], ident32[:])

        def gather(eng, key, h):
            words = rows_tile(key)[:, 2 * W * h : 2 * W * (h + 1)].bitcast(F32)
            if key[0] == "feat":
                dst = words.rearrange("p (r n u) -> p r n u", n=2, u=2)
                src = bank[key, h][:].rearrange("p (n u r) -> p r n u", n=2, u=2)
            else:
                dst = words.rearrange("p (n r u) -> p n r u", n=2, u=2)
                src = bank[key, h][:].rearrange("p (n u r) -> p n r u", n=2, u=2)
            copy_on(eng, dst, src)

        def trunk_mm(eng, c, g, lo, w, t):
            bank["z", c, g, lo, t] = new_bank()
            mx_pass(eng, bank["z", c, g, lo, t], ("trunk", 0, g), NP * t, ("feat", c), lo, w, True, True)

        def trunk_tanh(eng, c, g, lo, w, t):
            eng.activation(
                out=act_tile(("tanh", c, g))[:, t, lo : lo + w],
                in_=bank["z", c, g, lo, t][:, 0:w],
                func=ACT.Tanh,
                bias=tanh_bias[:, g, t : t + 1],
                scale=mode_vec[:, SLOPE + g, t : t + 1],
            )

        def branch_mm(eng, name, g, t):
            bank[name, g, t] = new_bank()
            for s in range(2):
                mx_pass(eng, bank[name, g, t], (name, s, g), NP * t, ("sens", s), 0, W, s == 0, s == 1)

        def gate(eng, g, t):
            bias = mode_vec[:, C_GATE + g, t : t + 1]
            eng.activation(out=act_tile(("gate", g))[:, t, :], in_=bank["gate", g, t][:], func=ACT.Sigmoid, bias=bias)

        def gate_value(eng, g, t):
            eng.scalar_tensor_tensor(
                out=rows_tile(("flat", g))[:, W * t : W * (t + 1)],
                in0=bank["val", g, t][:],
                scalar=mode_vec[:, C_VAL + g, t : t + 1],
                in1=act32["gate", g][:, t, :],
                op0=ALU.add,
                op1=ALU.mult,
            )

        def by_runs(ap, lo, w, run):
            return ap[:, :, lo : lo + w].rearrange("p t (m i) -> p m t i", i=run)

        def rows_by_runs(key, lo, w, run):
            return rows_tile(key)[:, 4 * lo : 4 * (lo + w)].rearrange("p (m i t) -> p m t i", i=run, t=4)

        def lay_beta(eng, g, t0, nt):
            flat = rows["flat", g][:].rearrange("p (t b) -> p t b", t=4)
            copy_on(eng, rows_by_runs(("beta", g), NP * t0, NP * nt, 4), by_runs(flat, NP * t0, NP * nt, 4))

        def make_tau(eng, c, g, lo, w):
            gain = bank["mode"][:, AMP + g : W : NP].unsqueeze(1).unsqueeze(3).broadcast_to([NP, w // 2, 4, 2])
            in0 = by_runs(act32["tanh", c, g], lo, w, 2)
            eng.tensor_tensor(out=rows_by_runs(("tau", c, g), lo, w, 2), in0=in0, in1=gain, op=ALU.mult)

        def share_tau(eng, c, g, lo, w, k):
            dst = rows_tile(("tau", c, g))[:, 4 * lo : 4 * (lo + w)].rearrange("p (q t) -> p q t", t=4)
            src = act32["tanh", c, g][:, :, lo : lo + w].rearrange("p t q -> p q t")
            gain = amp_copies[:, k, :].unsqueeze(1).broadcast_to([NP, w, 4])
            eng.tensor_tensor(out=dst, in0=src, in1=gain, op=ALU.mult)

        def field_mm(eng, n, lo, w):
            bank["field", n, lo] = new_bank()
            for g in range(2):
                mx_pass(eng, bank["field", n, lo], ("tau", n // 4, g), NP * (n % 4), ("beta", g), lo, w, g == 0, g == 1)

        def impose(eng, n, lo, w):
            if n not in turned:
                turned[n] = work.tile([NP, W], F32, name="turned", tag="turned", bufs=TURNED_BUFS)
            dst, src = turned[n][:, lo : lo + w], bank["field", n, lo][:, 0:w]
            gain, offset = dist_vec[:, n : n + 1], lift_vec[:, n : n + 1]
            if eng is scalar:
                eng.activation(out=dst, in_=src, func=ACT.Identity, bias=offset, scale=gain)
            else:
                eng.tensor_scalar(out=dst, in0=src, scalar1=gain, scalar2=offset, op0=ALU.mult, op1=ALU.add)

        def turn_back(eng, n0, nn, b0, nb):
            bank["out", n0, b0] = new_bank()
            for k in range(nb):
                for n in range(nn):
                    col = NP * (nn * k + n)
                    src = turned[n0 + n][:, NP * (b0 + k) : NP * (b0 + k + 1)]
                    eng.transpose(bank["out", n0, b0][:, col : col + NP], src, ident32[:])

        def unload(eng, n0, nn, b0, nb):
            result[n0, b0] = work.tile([NP, W], F32, name="result", tag="result", bufs=RESULT_BUFS)
            copy_on(eng, result[n0, b0][:, 0 : NP * nn * nb], bank["out", n0, b0][:, 0 : NP * nn * nb])

        def store(eng, n0, nn, b0, nb):
            dst = out[NP * b0 : NP * (b0 + nb), NP * n0 : NP * (n0 + nn)].rearrange("(k p) q -> p k q", p=NP)
            eng.dma_start(out=dst, in_=result[n0, b0][:, 0 : NP * nn * nb].rearrange("p (k q) -> p k q", k=nb))


        def four(fn, *args):
            return [(fn, *args, t) for t in range(4)]

        def halves(fn, *key):
            return [(fn, key, h) for h in range(2)]

        def lay(name, s, g, t0=0, nt=4):
            return (lay_weight, name, s, g, t0, nt)

        def quant(*key, lo=0, w=W):
            return (quantize, key, lo, w)

        def tau(c, g, lo=0, w=W):
            return (make_tau, c, g, lo, w)

        def tanhs(c, g, lo=0, w=W):
            return four(trunk_tanh, c, g, lo, w)

        def zs(c, g, lo=0, w=W):
            return four(trunk_mm, c, g, lo, w)

        def tiles(fn, n0, n1):
            return [(fn, n, 0, W) for n in range(n0, n1)]

        def quarters(key, ts, k):
            return [(lay_quarter, key, t, k) for t in ts]

        chunk_blocks = [[(4 * c, 4, b, 1) for b in range(4)] for c in range(3)]
        pair_blocks = [(12, 2, b, 2) for b in (0, 2)]
        last_blocks = [(14, 2, b, 1) for b in range(4)]

        def blocks(fn, which):
            return [(fn, *block) for block in which]


        sync_order = [(load_feat, 0, 0, 1), (load_feat, 0, 1, 1)]
        sync_order += [(load_mode_rows, row) for row in (C_TRUNK, SLOPE, AMP, C_VAL, C_GATE)]
        sync_order += [(load_weight, "trunk", 0, 0), (load_weight, "trunk", 0, 1), (load_weight, "gate", 0, 0)]
        sync_order += [(load_weight, "gate", 1, 0), (load_feat, 1, 0, 2), (load_weight, "val", 0, 0)]
        sync_order += [(load_query_rows, DIST), (load_weight, "gate", 0, 1), (load_sens, 0), (load_sens, 1)]
        sync_order += [(load_feat, 2, 0, 2), (load_weight, "val", 1, 0), (load_feat, 3, 0, 2), (load_query_rows, LIFT)]
        sync_order += [(load_weight, "gate", 1, 1), (load_weight, "val", 1, 1), (load_weight, "val", 0, 1)]
        for which in chunk_blocks + [pair_blocks, last_blocks]:
            sync_order += blocks(store, which)

        vector_order = [(clear, "mode"), (order_mode_rows,), (clear, "query"), lay("trunk", 0, 0, 2, 2), (make_tanh_bias,)]
        vector_order += [quant("feat", 0, w=HALF), quant("trunk", 0, 0, lo=HALF, w=HALF), quant("feat", 0, lo=HALF, w=HALF)]
        vector_order += [lay("trunk", 0, 1, 0, 2), quant("trunk", 0, 0, w=HALF), lay("gate", 0, 0), quant("trunk", 0, 1)]
        vector_order += [(release, 0), quant("gate", 0, 0), tau(0, 0)] + halves(gather, "feat", 1) + [tau(0, 1)]
        vector_order += [quant("feat", 1), quant("tau", 0, 1), quant("gate", 1, 0), quant("sens", 0), quant("val", 0, 0)]
        vector_order += [quant("sens", 1), lay("val", 1, 0)]
        vector_order += [(release, 1), quant("gate", 0, 1), tau(1, 0), quant("val", 1, 0), quant("gate", 1, 1)]
        vector_order += [(release, 2), quant("feat", 2)]
        for h in range(2):
            vector_order += [(gather, ("feat", 3), h)] + four(gate_value, 0)[2 * h : 2 * h + 2]
        vector_order += [tau(1, 1, HALF, HALF), quant("val", 0, 1), quant("val", 1, 1), quant("feat", 3)]
        vector_order += [(release, 3), quant("tau", 1, 0)] + four(gate_value, 1)
        vector_order += [quant("tau", 0, 0), (lay_beta, 1, 0, 4), quant("beta", 0)]
        vector_order += [(release_amp, 0, 1), quant("beta", 1), tau(2, 0)] + tiles(impose, 0, 1) + [quant("tau", 1, 1)]
        vector_order += [(release_amp, 1, 1), quant("tau", 2, 0), tau(2, 1, HALF, HALF)] + tiles(impose, 4, 7)
        vector_order += [(release_amp, 2, 1), quant("tau", 2, 1), tau(3, 0), quant("tau", 3, 0)]
        vector_order += [(release_amp, 3, 1), quant("tau", 3, 1, w=HALF)] + tiles(impose, 10, 13)
        vector_order += blocks(unload, chunk_blocks[2][:2])
        vector_order += [quant("tau", 3, 1, lo=2 * NP, w=NP), quant("tau", 3, 1, lo=3 * NP, w=NP)]
        vector_order += blocks(unload, pair_blocks[:1]) + tiles(impose, 14, 15)
        vector_order += [(impose, 15, 0, HALF), (impose, 15, HALF, HALF)] + blocks(unload, last_blocks[1::2])

        gpsimd_order = [(clear, "warm"), (identity, "float32"), (identity, "bfloat16")]
        gpsimd_order += quarters(("gate", 1, 0), range(4), 0) + quarters(("val", 0, 0), range(2), 0)
        gpsimd_order += quarters(("gate", 1, 1), range(2), 1)
        gpsimd_order += quarters(("val", 0, 1), range(1), 2) + quarters(("val", 1, 1), range(4), 2)
        gpsimd_order += quarters(("beta", 0), range(3), 3)
        gpsimd_order += [(share_tau, c, 1, 0, HALF, c - 1) for c in (1, 2, 3)]
        gpsimd_order += [(share_tau, 3, 1, NP * n, NP, 3) for n in (2, 3)]

        scalar_order = [(warm_up,)] + halves(gather, "feat", 0) + [(gather_mode,)]
        scalar_order += [lay("trunk", 0, 0, 0, 2), lay("trunk", 0, 1, 2, 2)]
        for ts in (slice(2, 4), slice(0, 2)):
            scalar_order += tanhs(0, 0, 0, HALF)[ts] + tanhs(0, 0, HALF, HALF)[ts]
        scalar_order += tanhs(0, 1) + [lay("val", 0, 0, 2, 2), lay("gate", 0, 1)]
        scalar_order += halves(gather, "sens", 0) + halves(gather, "sens", 1) + tanhs(1, 0)
        scalar_order += [(gather, ("feat", 2), 0), lay("gate", 1, 1, 2, 2), (gather, ("feat", 2), 1)]
        scalar_order += four(gate, 0)[:2] + tanhs(1, 1)[:2] + four(gate, 0)[2:] + tanhs(1, 1)[2:]
        scalar_order += [lay("val", 0, 1, 1, 3)] + four(gate, 1) + [(gather_query,)] + tanhs(2, 0) + [(lay_beta, 0, 3, 1)]
        scalar_order += tanhs(3, 1)[:2] + tanhs(2, 1)[:2] + tanhs(3, 1)[2:] + tanhs(3, 0)[:2] + tanhs(2, 1)[2:]
        scalar_order += tiles(impose, 1, 4) + tanhs(3, 0)[2:] + tiles(impose, 7, 8)
        scalar_order += blocks(unload, chunk_blocks[0] + chunk_blocks[1][:1]) + tiles(impose, 8, 10)
        scalar_order += blocks(unload, chunk_blocks[1][1:]) + tiles(impose, 13, 14)
        scalar_order += blocks(unload, chunk_blocks[2][2:] + pair_blocks[1:] + last_blocks[0::2])

        tensor_order = halves(turn, "feat", 0) + [(turn_mode_rows,)]
        for ts in (slice(2, 4), slice(0, 2)):
            tensor_order += zs(0, 0, 0, HALF)[ts] + zs(0, 0, HALF, HALF)[ts]
        tensor_order += zs(0, 1) + halves(turn, "feat", 1) + halves(turn, "sens", 0) + halves(turn, "sens", 1)
        tensor_order += zs(1, 0) + halves(turn, "feat", 2) + halves(turn, "feat", 3)
        tensor_order += four(branch_mm, "gate", 0)[:2] + zs(1, 1)[:2] + four(branch_mm, "gate", 0)[2:]
        tensor_order += four(branch_mm, "val", 0)[:2] + zs(1, 1)[2:] + four(branch_mm, "val", 0)[2:]
        tensor_order += zs(2, 0)[:2] + [(turn_query_rows,)] + four(branch_mm, "gate", 1) + zs(2, 0)[2:]
        tensor_order += four(branch_mm, "val", 1) + zs(3, 1)[:2] + zs(3, 0)[:2] + zs(3, 1)[2:] + zs(2, 1)
        tensor_order += tiles(field_mm, 0, 4) + zs(3, 0)[2:] + tiles(field_mm, 4, 8)
        tensor_order += blocks(turn_back, chunk_blocks[0] + chunk_blocks[1]) + tiles(field_mm, 8, 14)
        tensor_order += blocks(turn_back, chunk_blocks[2] + pair_blocks[:1]) + tiles(field_mm, 14, 15)
        tensor_order += [(field_mm, 15, 0, HALF)] + blocks(turn_back, pair_blocks[1:]) + [(field_mm, 15, HALF, HALF)]
        tensor_order += blocks(turn_back, last_blocks)


        programs = [
            (gpsimd, gpsimd_order),
            (sync, sync_order),
            (vector, vector_order),
            (scalar, scalar_order),
            (tensor, tensor_order),
        ]
        steps = [step for eng, order in programs for step in order]


        def covering(fn, key, lo, hi):
            n = len(key) + 1
            return [st for st in steps if st[0] is fn and st[1:n] == key and st[n] < hi and st[n] + st[n + 1] > lo]

        def quantized(key, lo=0, hi=W):
            return covering(quantize, (key,), lo, hi)

        def writers_of_rows(key, lo, w):
            kind = key[0]
            if kind in ("feat", "sens"):
                return [(gather, key, h) for h in range(lo // HALF, (lo + w) // HALF)]
            if kind == "tau":
                return covering(make_tau, key[1:], lo, lo + w) + covering(share_tau, key[1:], lo, lo + w)
            shared = [st for st in steps if st[0] is lay_quarter and st[1] == key and lo <= NP * st[2] < lo + w]
            if kind == "beta":
                return shared + covering(lay_beta, key[1:], lo // NP, (lo + w) // NP)
            return shared + covering(lay_weight, key, lo // NP, (lo + w) // NP)

        def unlaid(key):
            return four(gate_value, key[1]) if key[0] == "beta" else [(load_weight, *key)]

        def unturned(key, h):
            return covering(load_feat, key[1:], h, h + 1) if key[0] == "feat" else [(load_sens, h)]

        inputs = {
            load_query_rows: lambda row: [(clear, "query")],
            warm_up: lambda: [(clear, "warm")],
            order_mode_rows: lambda: [(clear, "mode")] + [st for st in steps if st[0] is load_mode_rows],
            turn_mode_rows: lambda: [(order_mode_rows,), (identity, "bfloat16")],
            gather_mode: lambda: [(turn_mode_rows,)],
            make_tanh_bias: lambda: [(gather_mode,)],
            turn_query_rows: lambda: [(load_query_rows, DIST), (load_query_rows, LIFT), (identity, "bfloat16")],
            gather_query: lambda: [(turn_query_rows,)],
            lay_weight: lambda name, s, g, t0, nt: [(load_weight, name, s, g)],
            release_amp: lambda k, g: [(gather_mode,)],
            lay_quarter: lambda key, t, k: [(release, k)] + unlaid(key),
            quantize: writers_of_rows,
            turn: lambda key, h: [(identity, "float32")] + unturned(key, h),
            gather: lambda key, h: [(turn, key, h)],
            trunk_mm: lambda c, g, lo, w, t: quantized(("trunk", 0, g), NP * t, NP * (t + 1))
            + quantized(("feat", c), lo, lo + w),
            trunk_tanh: lambda *args: [(trunk_mm, *args), (make_tanh_bias,)],
            branch_mm: lambda name, g, t: [
                st for s in range(2) for key in ((name, s, g), ("sens", s)) for st in quantized(key)
            ],
            gate: lambda g, t: [(branch_mm, "gate", g, t), (gather_mode,)],
            gate_value: lambda g, t: [(branch_mm, "val", g, t), (gate, g, t)],
            lay_beta: lambda g, t0, nt: four(gate_value, g),
            make_tau: lambda c, g, lo, w: [(gather_mode,)] + covering(trunk_tanh, (c, g), lo, lo + w),
            share_tau: lambda c, g, lo, w, k: [(release_amp, k, g)] + covering(trunk_tanh, (c, g), lo, lo + w),
            field_mm: lambda n, lo, w: [
                st
                for g in range(2)
                for st in quantized(("beta", g)) + quantized(("tau", n // 4, g), NP * (n % 4), NP * (n % 4 + 1))
            ],
            impose: lambda *args: [(field_mm, *args), (gather_query,)],
            turn_back: lambda n0, nn, b0, nb: [
                st for n in range(n0, n0 + nn) for st in covering(impose, (n,), NP * b0, NP * (b0 + nb))
            ],
            unload: lambda *args: [(turn_back, *args)],
            store: lambda *args: [(unload, *args)],
        }

        def ready(step):
            return step[0] not in inputs or all(st in traced for st in inputs[step[0]](*step[1:]))

        traced, place = set(), [0] * len(programs)
        while len(traced) < len(steps):
            before = len(traced)
            for e, (eng, order) in enumerate(programs):
                if place[e] < len(order) and ready(order[place[e]]):
                    step = order[place[e]]
                    step[0](eng, *step[1:])
                    traced.add(step)
                    place[e] += 1
            assert len(traced) > before, "the orders wait for each other"
